import numpy as np
import ml_dtypes


def mxq(x, axis, fmt="e4m3"):
    dtype, down = {"e4m3": (ml_dtypes.float8_e4m3fn, 7), "e5m2": (ml_dtypes.float8_e5m2, 14)}[fmt]
    v = np.moveaxis(np.asarray(x, np.float32).astype(ml_dtypes.bfloat16).astype(np.float64), axis, -1)
    blocks = v.reshape(v.shape[:-1] + (-1, 32))
    amax = np.abs(blocks).max(-1, keepdims=True)
    byte = np.maximum(np.where(amax > 0, np.frexp(amax)[1] - 1 + 127, 0) - down, 1)
    scale = np.exp2(byte - 127.0)
    codes = (blocks / scale).astype(np.float32).astype(dtype).astype(np.float64)
    return np.moveaxis((codes * scale).reshape(v.shape), -1, axis)


WIDE = False


def mx_kscale(k):
    if not WIDE:
        return np.ones(k)
    levels = np.array([10, -10, 5, -5, 0])
    if k % 512:
        return np.exp2(np.random.permutation(np.resize(levels, k // 32))).repeat(32)
    a = np.empty((k // 512, 16))
    for p in range(k // 512):
        a[p, :8] = np.random.permutation(np.resize(levels, 8))
        for g in range(8):
            far = levels[np.abs(levels - a[p, g]) >= 10]
            a[p, g + 8] = far[np.random.randint(len(far))]
    return np.exp2(a.ravel()).repeat(32)


def f64(x):
    return np.asarray(x).astype(np.float64)


def striped(idx):
    return np.tile(idx.reshape(-1, 16).T, (8, 1)).astype(np.uint16)


def unstriped(offs):
    return offs[:16].T.reshape(-1).astype(np.int64)


def pack_weight(w):
    k, n = w.shape
    w = f64(np.asarray(w, np.float32).astype(ml_dtypes.bfloat16)).reshape(k // 32, 32, n)
    amax = np.abs(w).max(1)
    byte = np.clip(np.where(amax > 0, np.frexp(amax)[1] - 1 + 127 - 7, 1), 1, 254)
    scaled = (w * np.exp2(127.0 - byte)[:, None, :]).reshape(k, n).astype(np.float32)
    words = np.ascontiguousarray(scaled.reshape(k // 512, 128, 4, n).transpose(0, 1, 3, 2)).astype(ml_dtypes.float8_e4m3fn).view(np.uint8)
    return words, np.ascontiguousarray(byte.astype(np.uint8).reshape(k // 512, 16, n))


def unpack_weight(words, scales):
    g, p, n, _ = words.shape
    vals = np.ascontiguousarray(words).view(ml_dtypes.float8_e4m3fn).astype(np.float64) * np.repeat(np.exp2(scales.astype(np.float64) - 127.0), 8, axis=1)[..., None]
    return vals.transpose(0, 1, 3, 2).reshape(g * 512, n)


E2M1 = np.array([0.0, 0.5, 1.0, 1.5, 2.0, 3.0, 4.0, 6.0, -0.0, -0.5, -1.0, -1.5, -2.0, -3.0, -4.0, -6.0])


def pack_fp4(w):
    k, n = w.shape
    w = f64(np.asarray(w, np.float32).astype(ml_dtypes.bfloat16)).reshape(k // 32, 32, n)
    amax = np.abs(w).max(1)
    mant, ex = np.frexp(amax / 6.0)
    byte = np.clip(np.where(amax > 0, np.where(mant > 0.5, ex, ex - 1) + 127, 1), 1, 254)
    scaled = (w * np.exp2(127.0 - byte)[:, None, :]).reshape(k, n).astype(np.float32)
    c = np.ascontiguousarray(scaled.reshape(k // 512, 128, 4, n).transpose(0, 1, 3, 2)).astype(ml_dtypes.float4_e2m1fn).view(np.uint8) & 0xF
    words = (c[..., 0::2] | (c[..., 1::2] << 4)).reshape(k // 512, 128, 2 * n)
    return np.ascontiguousarray(words), np.ascontiguousarray(byte.astype(np.uint8).reshape(k // 512, 16, n))


def unpack_fp4(words, scales):
    g, _, n = scales.shape
    words = np.ascontiguousarray(words).reshape(g, 128, n, 2)
    nib = np.empty((g, 128, n, 4), np.uint8)
    nib[..., 0::2] = words & 0xF
    nib[..., 1::2] = words >> 4
    vals = E2M1[nib] * np.repeat(np.exp2(scales.astype(np.float64) - 127.0), 8, axis=1)[..., None]
    return vals.transpose(0, 1, 3, 2).reshape(g * 512, n)


def gelu(v):
    return 0.5 * v * (1.0 + np.tanh(np.sqrt(2.0 / np.pi) * (v + 0.044715 * v**3)))


K, T, D, H, N = 1024, 512, 4, 512, 256
P = 2 ** 7


def setup_inputs():
    n = np.random.standard_normal
    s = mx_kscale(K)[:, None]
    u = mx_kscale(H)
    packed_xT = pack_weight(n((K, T)) * s)
    packed_w2 = pack_fp4(n((H, N)) / np.sqrt(H) / u[:, None])
    return {
        "x_words": packed_xT[0],
        "x_scales": packed_xT[1],
        "w1": (n((K, H)) / np.sqrt(K) / s * u).astype(np.float32),
        "w2_words": packed_w2[0],
        "w2_scales": packed_w2[1],
        "gate": (np.tile(np.random.uniform(0.2, 1.0, (D, 1, T)) / np.sqrt(D), (1, P, 1))).astype(np.float32),
        "pos1": striped(np.random.permutation(T)),
        "pos2": striped(np.random.permutation(T)),
        "pos3": striped(np.random.permutation(T)),
        "pos4": striped(np.random.permutation(T)),
    }


def reference(x_words, x_scales, w1, w2_words, w2_scales, gate, pos1, pos2, pos3, pos4):
    xq = unpack_weight(x_words, x_scales)
    h = gelu(mxq(f64(w1), 0, "e4m3").T @ xq)
    z = h - (h[:, unstriped(pos1)] * f64(gate)[0, :1] + h[:, unstriped(pos2)] * f64(gate)[1, :1] + h[:, unstriped(pos3)] * f64(gate)[2, :1] + h[:, unstriped(pos4)] * f64(gate)[3, :1])
    return unpack_fp4(w2_words, w2_scales).T @ mxq(z, 0, "e4m3")

@@ -1,0 +1,213 @@
+from contextlib import ExitStack
+
+import concourse.mybir as mybir
+from concourse.masks import make_identity
+
+K, T, D, H, N = 1024, 512, 4, 512, 256
+FLOPS = 2 * K * H * T + 2 * H * N * T
+BYTES = K * T + K * T // 32 + 4 * K * H + H * N // 2 + H * N // 32 + 4 * D * T + D * 128 * 64 + 4 * N * T
+
+F32 = mybir.dt.float32
+BF16 = mybir.dt.bfloat16
+I32 = mybir.dt.int32
+U32 = mybir.dt.uint32
+U16 = mybir.dt.uint16
+U8 = mybir.dt.uint8
+FP8X4 = mybir.dt.float8_e4m3fn_x4
+FP4X4 = mybir.dt.float4_e2m1fn_x4
+GELU = mybir.ActivationFunctionType.Gelu_apprx_tanh
+COPY = mybir.ActivationFunctionType.Copy
+MULT = mybir.AluOpType.mult
+
+P = 128
+PACK = 4
+PASSES = K // (P * PACK)
+BLOCKS = H // P
+SPARE = 8
+
+
+def tile_picked_wlapl_gelu_l_kernel(
+    tc, x_words, x_scales, w1, w2_words, w2_scales, gate, pos1, pos2, pos3, pos4, out
+):
+    nc = tc.nc
+    with ExitStack() as ctx:
+        keep = ctx.enter_context(tc.tile_pool(name="keep", bufs=1))
+        psum = ctx.enter_context(tc.psum_pool(name="psum", bufs=1))
+
+        lists = [keep.tile([P, T // 16], U16, name=f"list{d}") for d in range(D)]
+        gates = [keep.tile([P, T], F32, name=f"gate{d}") for d in range(D)]
+        x_codes = [keep.tile([P, T], U32, name=f"x_codes{g}", align_bytes=64) for g in range(PASSES)]
+        zero_bias = keep.tile([P, 1], F32, tag="slot1", align_bytes=64)
+        planes = keep.tile([P, PASSES * T], U8, align_bytes=64)
+        w2_plane = keep.tile([P, N], U8, align_bytes=64)
+        w2_codes = keep.tile([P, 2 * N], U8, align_bytes=64)
+        ident = keep.tile([P, P], F32)
+        h = [keep.tile([P, T + SPARE if c < 2 else T], F32, name=f"h{c}") for c in range(BLOCKS)]
+        neg_h = [keep.tile([P, T], F32, name=f"neg_h{c}") for c in range(BLOCKS)]
+        zt_bf = [keep.tile([P, H], BF16, name=f"zt_bf{b}") for b in range(T // P)]
+        zt = [psum.tile([P, H], F32, name=f"zt{b}") for b in range(T // P)]
+
+        nc.gpsimd.memset(planes[:].bitcast(I32), 0)
+        nc.vector.memset(w2_plane[:].bitcast(I32), 0)
+        nc.vector.memset(zero_bias[:], 0.0)
+        make_identity(nc, ident[:])
+
+        w1_rows = w1.rearrange("(g p j) c -> g p j c", p=P, j=PACK)
+        w1_raw = {}
+
+        def load_w1(c0, width, passes=range(PASSES)):
+            for g in passes:
+                raw = keep.tile([P, PACK, width * P], F32, name=f"w1_raw{c0}_{g}", tag=f"w1_raw{min(c0, 1)}_{g}")
+                nc.sync.dma_start(out=raw[:], in_=w1_rows[g][:, :, c0 * P : (c0 + width) * P])
+                for c in range(c0, c0 + width):
+                    w1_raw[(c, g)] = raw[:, :, (c - c0) * P : (c - c0 + 1) * P]
+
+        x_planes = planes[:].bitcast(I32).rearrange("p (g w) -> p g w", g=PASSES)
+        x_scale_rows = x_scales.bitcast(I32).rearrange("g (q r) w -> r q g w", r=4)
+        positions = (pos1, pos2, pos3, pos4)
+
+        def load_x(g):
+            nc.sync.dma_start(
+                out=x_codes[g][:].bitcast(I32), in_=x_words[g].rearrange("p n t -> p (n t)").bitcast(I32)
+            )
+
+        load_w1(0, 1, [0])
+        for r in range(4):
+            nc.sync.dma_start(out=x_planes[r:P:32], in_=x_scale_rows[r])
+        load_x(0)
+        load_w1(0, 1, [1])
+        load_x(1)
+        nc.sync.dma_start(lists[0][:], positions[0])
+        nc.sync.dma_start(out=gates[0][:], in_=gate[0])
+        load_w1(1, 1)
+        for d in range(1, D):
+            nc.sync.dma_start(lists[d][:], positions[d])
+            nc.sync.dma_start(out=gates[d][:], in_=gate[d])
+        load_w1(2, 2)
+        nc.sync.dma_start(out=w2_codes[:].bitcast(I32), in_=w2_words[0].bitcast(I32))
+        w2_scale_rows = w2_scales[0].bitcast(I32).rearrange("(q r) w -> r q w", r=4)
+        for r in range(4):
+            nc.sync.dma_start(out=w2_plane[:].bitcast(I32)[r:P:32], in_=w2_scale_rows[r])
+
+        for c in range(2):
+            nc.scalar.activation(out=h[c][:, T:], in_=ident[:, :SPARE], func=GELU)
+
+        def project(c):
+            grouped = keep.tile([P, PASSES * P * PACK], BF16, name=f"w1_bf{c}", tag=f"slot{c}", align_bytes=64)
+            codes = keep.tile([P, PASSES * P], U32, name=f"w1_codes{c}", align_bytes=64)
+            scales = keep.tile([P, PASSES * P], U8, name=f"w1_scales{c}", align_bytes=64)
+            copy = nc.vector.tensor_copy if c == 0 else nc.scalar.copy
+            for g in range(PASSES):
+                half = grouped[:, g * P * PACK : (g + 1) * P * PACK]
+                copy(
+                    out=half.rearrange("p (c i t) -> p c t i", i=4, t=PACK),
+                    in_=w1_raw[(c, g)].rearrange("p t (c i) -> p c t i", i=4),
+                )
+                if c == 0:
+                    cols = slice(g * P, (g + 1) * P)
+                    nc.vector.quantize_mx(out=codes[:, cols].bitcast(FP8X4), scales=scales[:, cols], in_=half)
+            if c > 0:
+                nc.vector.quantize_mx(out=codes[:].bitcast(FP8X4), scales=scales[:], in_=grouped[:])
+            u = psum.tile([P, T], F32, name=f"u{c}", tag="acc", bufs=2)
+            for g in range(PASSES):
+                cols = slice(g * P, (g + 1) * P)
+                nc.tensor.matmul_mx(
+                    out=u[:],
+                    lhsT=codes[:, cols].bitcast(FP8X4),
+                    lhsT_scale=scales[:, cols],
+                    rhs=x_codes[g][:].bitcast(FP8X4),
+                    rhs_scale=planes[:, g * T : (g + 1) * T],
+                    start=(g == 0),
+                    stop=(g == PASSES - 1),
+                )
+            nc.scalar.activation(out=h[c][:, :T], in_=u[:], func=GELU, bias=zero_bias[:] if c == 0 else 0.0)
+
+        def negate(c):
+            nc.scalar.activation(out=neg_h[c][:], in_=h[c][:, :T], func=COPY, scale=-1.0)
+
+        def neighbours(c, v0, width, tags):
+            blocks = range(v0 // P, (v0 + width) // P)
+            cols = slice(c * P, (c + 1) * P)
+            for d in range(D):
+                name = f"prod{c}_{v0}_{d}"
+                prod = keep.tile([P, width], F32, name=name, tag=tags.get(d, name), align_bytes=64)
+                nc.vector.tensor_tensor(
+                    prod[:],
+                    h[c][:].indirect(lists[d][:, v0 // 16 : (v0 + width) // 16]),
+                    gates[d][:, v0 : v0 + width],
+                    MULT,
+                )
+                for b in blocks:
+                    nc.tensor.matmul(
+                        zt[b][:, cols], prod[:, b * P - v0 : (b + 1) * P - v0], ident[:],
+                        start=(d == 0), stop=(d == D - 1), is_transpose=True,
+                    )
+                if d == D - 2:
+                    for b in blocks:
+                        nc.tensor.matmul(
+                            zt[b][:, cols], neg_h[c][:, b * P : (b + 1) * P], ident[:],
+                            start=False, stop=False, is_transpose=True,
+                        )
+
+        def round_z(c0, count, v0, width):
+            for b in range(v0 // P, (v0 + width) // P):
+                nc.scalar.activation(
+                    out=zt_bf[b][:].rearrange("v (u p e) -> v u p e", u=2, e=2)[:, :, 32 * c0 : 32 * (c0 + count), :],
+                    in_=zt[b][:, c0 * P : (c0 + count) * P].rearrange("v (q u e) -> v u q e", u=2, e=2),
+                    func=COPY,
+                    scale=-1.0,
+                )
+
+        def finish(v0, width, copy_out):
+            nb = width // P
+            turned = psum.tile([P, nb, 2, P], F32, name=f"turned{v0}", tag="turned", bufs=2)
+            for b in range(nb):
+                words = zt_bf[v0 // P + b][:].bitcast(F32)
+                for u in range(2):
+                    nc.tensor.transpose(turned[:, b, u, :], words[:, u * P : (u + 1) * P], ident[:])
+            z_bf = keep.tile([P, width * PACK], BF16, name=f"z_bf{v0}", tag=f"zslot{v0}", align_bytes=64)
+            nc.scalar.copy(
+                out=z_bf[:].bitcast(F32).rearrange("p (b v u) -> p b v u", b=nb, u=2),
+                in_=turned[:].rearrange("p b u v -> p b v u"),
+            )
+            z_codes = keep.tile([P, width], U32, name=f"z_codes{v0}", align_bytes=64)
+            z_scales = keep.tile([P, width], U8, name=f"z_scales{v0}", align_bytes=64)
+            nc.vector.quantize_mx(out=z_codes[:].bitcast(FP8X4), scales=z_scales[:], in_=z_bf[:])
+            acc = psum.tile([P, 2, width], F32, name=f"out_acc{v0}", tag="acc", bufs=2)
+            for m in range(N // P):
+                nc.tensor.matmul_mx(
+                    out=acc[:, m, :],
+                    lhsT=w2_codes[:, 2 * P * m : 2 * P * (m + 1)].bitcast(FP4X4),
+                    lhsT_scale=w2_plane[:, P * m : P * (m + 1)],
+                    rhs=z_codes[:].bitcast(FP8X4),
+                    rhs_scale=z_scales[:],
+                    start=True,
+                    stop=True,
+                )
+            result = keep.tile([P, 2, width], F32, name=f"result{v0}")
+            copy_out(out=result[:], in_=acc[:])
+            nc.sync.dma_start(
+                out=out.rearrange("(m p) v -> p m v", p=P)[:, :, v0 : v0 + width], in_=result[:]
+            )
+
+        project(0)
+        project(1)
+        negate(0)
+        neighbours(0, 0, T, {2: "slot1"})
+        project(2)
+        negate(1)
+        project(3)
+        negate(2)
+        negate(3)
+        neighbours(1, 0, T, {2: "slot2"})
+        round_z(0, 2, 0, T)
+        for v0, width, tags2, tags3, copy_out in (
+            (0, 256, {0: "slot3"}, {}, nc.scalar.copy),
+            (256, 128, {}, {}, nc.vector.tensor_copy),
+            (384, 128, {2: "zslot0"}, {}, nc.scalar.copy),
+        ):
+            neighbours(2, v0, width, tags2)
+            round_z(2, 1, v0, width)
+            neighbours(3, v0, width, tags3)
+            round_z(3, 1, v0, width)
+            finish(v0, width, copy_out)

@@ -35,10 +35,10 @@ def tile_picked_wlapl_gelu_l_kernel(
         psum = ctx.enter_context(tc.psum_pool(name="psum", bufs=1))
 
         lists = [keep.tile([P, T // 16], U16, name=f"list{d}") for d in range(D)]
-        gates = [keep.tile([P, T], F32, name=f"gate{d}") for d in range(D)]
-        x_codes = [keep.tile([P, T], U32, name=f"x_codes{g}", align_bytes=64) for g in range(PASSES)]
-        zero_bias = keep.tile([P, 1], F32, tag="slot1", align_bytes=64)
-        planes = keep.tile([P, PASSES * T], U8, align_bytes=64)
+        gates = [keep.tile([P, T], F32, name=f"gate{d}", align_bytes=256) for d in range(D)]
+        x_codes = [keep.tile([P, T], U32, name=f"x_codes{g}", align_bytes=256) for g in range(PASSES)]
+        zero_bias = keep.tile([P, 1], F32, tag="ring2", align_bytes=64)
+        planes = keep.tile([P, PASSES * T], U8, align_bytes=256)
         w2_plane = keep.tile([P, N], U8, align_bytes=64)
         w2_codes = keep.tile([P, 2 * N], U8, align_bytes=64)
         ident = keep.tile([P, P], F32)
@@ -57,7 +57,7 @@ def tile_picked_wlapl_gelu_l_kernel(
 
         def load_w1(c0, width, passes=range(PASSES)):
             for g in passes:
-                raw = keep.tile([P, PACK, width * P], F32, name=f"w1_raw{c0}_{g}", tag=f"w1_raw{min(c0, 1)}_{g}")
+                raw = keep.tile([P, PACK, width * P], F32, name=f"w1_raw{c0}_{g}", tag=f"w1_raw{c0 % 2}_{g}", align_bytes=256)
                 nc.sync.dma_start(out=raw[:], in_=w1_rows[g][:, :, c0 * P : (c0 + width) * P])
                 for c in range(c0, c0 + width):
                     w1_raw[(c, g)] = raw[:, :, (c - c0) * P : (c - c0 + 1) * P]
@@ -74,8 +74,8 @@ def tile_picked_wlapl_gelu_l_kernel(
         load_w1(0, 1, [0])
         for r in range(4):
             nc.sync.dma_start(out=x_planes[r:P:32], in_=x_scale_rows[r])
-        load_x(0)
         load_w1(0, 1, [1])
+        load_x(0)
         load_x(1)
         nc.sync.dma_start(lists[0][:], positions[0])
         nc.sync.dma_start(out=gates[0][:], in_=gate[0])
@@ -83,18 +83,13 @@ def tile_picked_wlapl_gelu_l_kernel(
         for d in range(1, D):
             nc.sync.dma_start(lists[d][:], positions[d])
             nc.sync.dma_start(out=gates[d][:], in_=gate[d])
-        load_w1(2, 2)
-        nc.sync.dma_start(out=w2_codes[:].bitcast(I32), in_=w2_words[0].bitcast(I32))
-        w2_scale_rows = w2_scales[0].bitcast(I32).rearrange("(q r) w -> r q w", r=4)
-        for r in range(4):
-            nc.sync.dma_start(out=w2_plane[:].bitcast(I32)[r:P:32], in_=w2_scale_rows[r])
 
         for c in range(2):
             nc.scalar.activation(out=h[c][:, T:], in_=ident[:, :SPARE], func=GELU)
 
         def project(c):
-            grouped = keep.tile([P, PASSES * P * PACK], BF16, name=f"w1_bf{c}", tag=f"slot{c}", align_bytes=64)
-            codes = keep.tile([P, PASSES * P], U32, name=f"w1_codes{c}", align_bytes=64)
+            grouped = keep.tile([P, PASSES * P * PACK], BF16, name=f"w1_bf{c}", tag=("w1_bf0", "ring2", "ring5", "ring1")[c], align_bytes=64)
+            codes = keep.tile([P, PASSES * P], U32, name=f"w1_codes{c}", tag="ring3" if c == 1 else f"w1_codes{c}", align_bytes=64)
             scales = keep.tile([P, PASSES * P], U8, name=f"w1_scales{c}", align_bytes=64)
             copy = nc.vector.tensor_copy if c == 0 else nc.scalar.copy
             for g in range(PASSES):
@@ -108,29 +103,37 @@ def tile_picked_wlapl_gelu_l_kernel(
                     nc.vector.quantize_mx(out=codes[:, cols].bitcast(FP8X4), scales=scales[:, cols], in_=half)
             if c > 0:
                 nc.vector.quantize_mx(out=codes[:].bitcast(FP8X4), scales=scales[:], in_=grouped[:])
-            u = psum.tile([P, T], F32, name=f"u{c}", tag="acc", bufs=2)
+            halves = [slice(s * T // 2, (s + 1) * T // 2) for s in range(2)]
+            u = [psum.tile([P, T // 2], F32, name=f"u{c}_{s}", tag="acc", bufs=2) for s in range(2)]
             for g in range(PASSES):
                 cols = slice(g * P, (g + 1) * P)
-                nc.tensor.matmul_mx(
-                    out=u[:],
-                    lhsT=codes[:, cols].bitcast(FP8X4),
-                    lhsT_scale=scales[:, cols],
-                    rhs=x_codes[g][:].bitcast(FP8X4),
-                    rhs_scale=planes[:, g * T : (g + 1) * T],
-                    start=(g == 0),
-                    stop=(g == PASSES - 1),
+                for s in range(2):
+                    nc.tensor.matmul_mx(
+                        out=u[s][:],
+                        lhsT=codes[:, cols].bitcast(FP8X4),
+                        lhsT_scale=scales[:, cols],
+                        rhs=x_codes[g][:, halves[s]].bitcast(FP8X4),
+                        rhs_scale=planes[:, g * T : (g + 1) * T][:, halves[s]],
+                        start=(g == 0),
+                        stop=(g == PASSES - 1),
+                    )
+            for s in range(2):
+                nc.scalar.activation(
+                    out=h[c][:, halves[s]], in_=u[s][:], func=GELU, bias=zero_bias[:] if c == 0 else 0.0
                 )
-            nc.scalar.activation(out=h[c][:, :T], in_=u[:], func=GELU, bias=zero_bias[:] if c == 0 else 0.0)
+
+        issued = []
 
         def negate(c):
             nc.scalar.activation(out=neg_h[c][:], in_=h[c][:, :T], func=COPY, scale=-1.0)
 
-        def neighbours(c, v0, width, tags):
+        def neighbours(c, v0, width):
             blocks = range(v0 // P, (v0 + width) // P)
             cols = slice(c * P, (c + 1) * P)
             for d in range(D):
                 name = f"prod{c}_{v0}_{d}"
-                prod = keep.tile([P, width], F32, name=name, tag=tags.get(d, name), align_bytes=64)
+                prod = keep.tile([P, width], F32, name=name, tag=f"ring{len(issued) % 6}", align_bytes=64)
+                issued.append(name)
                 nc.vector.tensor_tensor(
                     prod[:],
                     h[c][:].indirect(lists[d][:, v0 // 16 : (v0 + width) // 16]),
@@ -165,7 +168,7 @@ def tile_picked_wlapl_gelu_l_kernel(
                 words = zt_bf[v0 // P + b][:].bitcast(F32)
                 for u in range(2):
                     nc.tensor.transpose(turned[:, b, u, :], words[:, u * P : (u + 1) * P], ident[:])
-            z_bf = keep.tile([P, width * PACK], BF16, name=f"z_bf{v0}", tag=f"zslot{v0}", align_bytes=64)
+            z_bf = keep.tile([P, width * PACK], BF16, name=f"z_bf{v0}", align_bytes=64)
             nc.scalar.copy(
                 out=z_bf[:].bitcast(F32).rearrange("p (b v u) -> p b v u", b=nb, u=2),
                 in_=turned[:].rearrange("p b u v -> p b v u"),
@@ -173,10 +176,11 @@ def tile_picked_wlapl_gelu_l_kernel(
             z_codes = keep.tile([P, width], U32, name=f"z_codes{v0}", align_bytes=64)
             z_scales = keep.tile([P, width], U8, name=f"z_scales{v0}", align_bytes=64)
             nc.vector.quantize_mx(out=z_codes[:].bitcast(FP8X4), scales=z_scales[:], in_=z_bf[:])
-            acc = psum.tile([P, 2, width], F32, name=f"out_acc{v0}", tag="acc", bufs=2)
+            result = keep.tile([P, 2, width], F32, name=f"result{v0}", align_bytes=256)
             for m in range(N // P):
+                acc = psum.tile([P, width], F32, name=f"out_acc{v0}_{m}", tag="acc", bufs=2)
                 nc.tensor.matmul_mx(
-                    out=acc[:, m, :],
+                    out=acc[:],
                     lhsT=w2_codes[:, 2 * P * m : 2 * P * (m + 1)].bitcast(FP4X4),
                     lhsT_scale=w2_plane[:, P * m : P * (m + 1)],
                     rhs=z_codes[:].bitcast(FP8X4),
@@ -184,8 +188,7 @@ def tile_picked_wlapl_gelu_l_kernel(
                     start=True,
                     stop=True,
                 )
-            result = keep.tile([P, 2, width], F32, name=f"result{v0}")
-            copy_out(out=result[:], in_=acc[:])
+                copy_out[m](out=result[:, m, :], in_=acc[:])
             nc.sync.dma_start(
                 out=out.rearrange("(m p) v -> p m v", p=P)[:, :, v0 : v0 + width], in_=result[:]
             )
@@ -193,21 +196,32 @@ def tile_picked_wlapl_gelu_l_kernel(
         project(0)
         project(1)
         negate(0)
-        neighbours(0, 0, T, {2: "slot1"})
+        load_w1(2, 1)
+        load_w1(3, 1)
+        nc.sync.dma_start(out=w2_codes[:].bitcast(I32), in_=w2_words[0].bitcast(I32))
+        w2_scale_rows = w2_scales[0].bitcast(I32).rearrange("(q r) w -> r q w", r=4)
+        for r in range(4):
+            nc.sync.dma_start(out=w2_plane[:].bitcast(I32)[r:P:32], in_=w2_scale_rows[r])
+        neighbours(0, 0, T)
         project(2)
         negate(1)
         project(3)
         negate(2)
         negate(3)
-        neighbours(1, 0, T, {2: "slot2"})
+        neighbours(1, 0, T)
         round_z(0, 2, 0, T)
-        for v0, width, tags2, tags3, copy_out in (
-            (0, 256, {0: "slot3"}, {}, nc.scalar.copy),
-            (256, 128, {}, {}, nc.vector.tensor_copy),
-            (384, 128, {2: "zslot0"}, {}, nc.scalar.copy),
-        ):
-            neighbours(2, v0, width, tags2)
-            round_z(2, 1, v0, width)
-            neighbours(3, v0, width, tags3)
-            round_z(3, 1, v0, width)
-            finish(v0, width, copy_out)
+        half, quarter = T // 2, T // 4
+        for v0 in (0, half):
+            neighbours(2, v0, half)
+            round_z(2, 1, v0, half)
+            if v0 == 0:
+                pieces = ((0, half, (nc.scalar.copy, nc.scalar.copy)),)
+            else:
+                pieces = (
+                    (half, quarter, (nc.vector.tensor_copy, nc.vector.tensor_copy)),
+                    (half + quarter, quarter, (nc.scalar.copy, nc.vector.tensor_copy)),
+                )
+            for v1, width, copy_out in pieces:
+                neighbours(3, v1, width)
+                round_z(3, 1, v1, width)
+                finish(v1, width, copy_out)

@@ -23,7 +23,9 @@ P = 128
 PACK = 4
 PASSES = K // (P * PACK)
 BLOCKS = H // P
+HALF, QUARTER = T // 2, T // 4
 SPARE = 8
+RING = 7
 
 
 def tile_picked_wlapl_gelu_l_kernel(
@@ -32,151 +34,165 @@ def tile_picked_wlapl_gelu_l_kernel(
     nc = tc.nc
     with ExitStack() as ctx:
         keep = ctx.enter_context(tc.tile_pool(name="keep", bufs=1))
+        late = ctx.enter_context(tc.tile_pool(name="late", bufs=1))
         psum = ctx.enter_context(tc.psum_pool(name="psum", bufs=1))
+
+        def ring_tile(shape, dtype, name, slot):
+            return keep.tile(shape, dtype, name=name, tag=f"ring{slot}", align_bytes=64)
 
         lists = [keep.tile([P, T // 16], U16, name=f"list{d}") for d in range(D)]
         gates = [keep.tile([P, T], F32, name=f"gate{d}", align_bytes=256) for d in range(D)]
         x_codes = [keep.tile([P, T], U32, name=f"x_codes{g}", align_bytes=256) for g in range(PASSES)]
-        zero_bias = keep.tile([P, 1], F32, tag="ring2", align_bytes=64)
-        planes = keep.tile([P, PASSES * T], U8, align_bytes=256)
-        w2_plane = keep.tile([P, N], U8, align_bytes=64)
+        x_planes = keep.tile([P, PASSES * T], U8, align_bytes=256)
         w2_codes = keep.tile([P, 2 * N], U8, align_bytes=64)
+        w2_plane = keep.tile([P, N], U8, align_bytes=64)
         ident = keep.tile([P, P], F32)
         h = [keep.tile([P, T + SPARE if c < 2 else T], F32, name=f"h{c}") for c in range(BLOCKS)]
         neg_h = [keep.tile([P, T], F32, name=f"neg_h{c}") for c in range(BLOCKS)]
-        zt_bf = [keep.tile([P, H], BF16, name=f"zt_bf{b}") for b in range(T // P)]
         zt = [psum.tile([P, H], F32, name=f"zt{b}") for b in range(T // P)]
+        zt_bf = [keep.tile([P, H], BF16, name=f"zt_bf{b}") for b in range(T // P)]
 
-        nc.gpsimd.memset(planes[:].bitcast(I32), 0)
+        grouped_slot = {1: 2, 2: 6, 3: 0}
+        codes_slot = {1: 3}
+        bias = {c: ring_tile([P, 1], F32, f"bias{c}", grouped_slot[c + 1]) for c in range(2)}
+
+        nc.gpsimd.memset(x_planes[:].bitcast(I32), 0)
         nc.vector.memset(w2_plane[:].bitcast(I32), 0)
-        nc.vector.memset(zero_bias[:], 0.0)
+        for c in bias:
+            nc.vector.memset(bias[c][:], 0.0)
         make_identity(nc, ident[:])
 
-        w1_rows = w1.rearrange("(g p j) c -> g p j c", p=P, j=PACK)
+        w1_rows = w1.rearrange("(g p j) i -> g p j i", p=P, j=PACK)
         w1_raw = {}
 
-        def load_w1(c0, width, passes=range(PASSES)):
-            for g in passes:
-                raw = keep.tile([P, PACK, width * P], F32, name=f"w1_raw{c0}_{g}", tag=f"w1_raw{c0 % 2}_{g}", align_bytes=256)
-                nc.sync.dma_start(out=raw[:], in_=w1_rows[g][:, :, c0 * P : (c0 + width) * P])
-                for c in range(c0, c0 + width):
-                    w1_raw[(c, g)] = raw[:, :, (c - c0) * P : (c - c0 + 1) * P]
+        def load_w1(c, g):
+            raw = keep.tile([P, PACK, P], F32, name=f"w1_raw{c}_{g}", tag=f"w1_raw{c % 2}_{g}", align_bytes=256)
+            nc.sync.dma_start(out=raw[:], in_=w1_rows[g][:, :, c * P : (c + 1) * P])
+            w1_raw[(c, g)] = raw
 
-        x_planes = planes[:].bitcast(I32).rearrange("p (g w) -> p g w", g=PASSES)
+        def load_neighbours(d):
+            nc.sync.dma_start(lists[d][:], (pos1, pos2, pos3, pos4)[d])
+            nc.sync.dma_start(out=gates[d][:], in_=gate[d])
+
+        load_w1(0, 0)
+        x_plane_words = x_planes[:].bitcast(I32).rearrange("p (g w) -> p g w", g=PASSES)
         x_scale_rows = x_scales.bitcast(I32).rearrange("g (q r) w -> r q g w", r=4)
-        positions = (pos1, pos2, pos3, pos4)
-
-        def load_x(g):
+        for r in range(4):
+            nc.sync.dma_start(out=x_plane_words[r:P:32], in_=x_scale_rows[r])
+        load_w1(0, 1)
+        for g in range(PASSES):
             nc.sync.dma_start(
                 out=x_codes[g][:].bitcast(I32), in_=x_words[g].rearrange("p n t -> p (n t)").bitcast(I32)
             )
-
-        load_w1(0, 1, [0])
-        for r in range(4):
-            nc.sync.dma_start(out=x_planes[r:P:32], in_=x_scale_rows[r])
-        load_w1(0, 1, [1])
-        load_x(0)
-        load_x(1)
-        nc.sync.dma_start(lists[0][:], positions[0])
-        nc.sync.dma_start(out=gates[0][:], in_=gate[0])
-        load_w1(1, 1)
+        load_neighbours(0)
+        for g in range(PASSES):
+            load_w1(1, g)
         for d in range(1, D):
-            nc.sync.dma_start(lists[d][:], positions[d])
-            nc.sync.dma_start(out=gates[d][:], in_=gate[d])
+            load_neighbours(d)
 
         for c in range(2):
             nc.scalar.activation(out=h[c][:, T:], in_=ident[:, :SPARE], func=GELU)
 
         def project(c):
-            grouped = keep.tile([P, PASSES * P * PACK], BF16, name=f"w1_bf{c}", tag=("w1_bf0", "ring2", "ring5", "ring1")[c], align_bytes=64)
-            codes = keep.tile([P, PASSES * P], U32, name=f"w1_codes{c}", tag="ring3" if c == 1 else f"w1_codes{c}", align_bytes=64)
+            width = P * PACK
+            if c in grouped_slot:
+                grouped = ring_tile([P, PASSES * width], BF16, f"w1_bf{c}", grouped_slot[c])
+            else:
+                grouped = keep.tile([P, PASSES * width], BF16, name=f"w1_bf{c}", align_bytes=64)
+            if c in codes_slot:
+                codes = ring_tile([P, PASSES * P], U32, f"w1_codes{c}", codes_slot[c])
+            else:
+                codes = keep.tile([P, PASSES * P], U32, name=f"w1_codes{c}", align_bytes=64)
             scales = keep.tile([P, PASSES * P], U8, name=f"w1_scales{c}", align_bytes=64)
-            copy = nc.vector.tensor_copy if c == 0 else nc.scalar.copy
+            first = c == 0
+            cast = nc.vector.tensor_copy if first else nc.scalar.copy
             for g in range(PASSES):
-                half = grouped[:, g * P * PACK : (g + 1) * P * PACK]
-                copy(
-                    out=half.rearrange("p (c i t) -> p c t i", i=4, t=PACK),
-                    in_=w1_raw[(c, g)].rearrange("p t (c i) -> p c t i", i=4),
+                part = grouped[:, g * width : (g + 1) * width]
+                cast(
+                    out=part.rearrange("p (a n t) -> p a t n", n=4, t=PACK),
+                    in_=w1_raw[(c, g)][:].rearrange("p t (a n) -> p a t n", n=4),
                 )
-                if c == 0:
+                if first:
                     cols = slice(g * P, (g + 1) * P)
-                    nc.vector.quantize_mx(out=codes[:, cols].bitcast(FP8X4), scales=scales[:, cols], in_=half)
-            if c > 0:
+                    nc.vector.quantize_mx(out=codes[:, cols].bitcast(FP8X4), scales=scales[:, cols], in_=part)
+            if not first:
                 nc.vector.quantize_mx(out=codes[:].bitcast(FP8X4), scales=scales[:], in_=grouped[:])
-            halves = [slice(s * T // 2, (s + 1) * T // 2) for s in range(2)]
-            u = [psum.tile([P, T // 2], F32, name=f"u{c}_{s}", tag="acc", bufs=2) for s in range(2)]
+            halves = [slice(s * HALF, (s + 1) * HALF) for s in range(2)]
+            pre = [psum.tile([P, HALF], F32, name=f"pre{c}_{s}", tag="acc", bufs=2) for s in range(2)]
             for g in range(PASSES):
                 cols = slice(g * P, (g + 1) * P)
                 for s in range(2):
                     nc.tensor.matmul_mx(
-                        out=u[s][:],
+                        out=pre[s][:],
                         lhsT=codes[:, cols].bitcast(FP8X4),
                         lhsT_scale=scales[:, cols],
                         rhs=x_codes[g][:, halves[s]].bitcast(FP8X4),
-                        rhs_scale=planes[:, g * T : (g + 1) * T][:, halves[s]],
+                        rhs_scale=x_planes[:, g * T : (g + 1) * T][:, halves[s]],
                         start=(g == 0),
                         stop=(g == PASSES - 1),
                     )
             for s in range(2):
                 nc.scalar.activation(
-                    out=h[c][:, halves[s]], in_=u[s][:], func=GELU, bias=zero_bias[:] if c == 0 else 0.0
+                    out=h[c][:, halves[s]], in_=pre[s][:], func=GELU, bias=bias[c][:] if c in bias else 0.0
                 )
-
-        issued = []
 
         def negate(c):
             nc.scalar.activation(out=neg_h[c][:], in_=h[c][:, :T], func=COPY, scale=-1.0)
 
-        def neighbours(c, v0, width):
-            blocks = range(v0 // P, (v0 + width) // P)
+        def neighbours(c, v0, width, product_tile):
+            banks = range(v0 // P, (v0 + width) // P)
             cols = slice(c * P, (c + 1) * P)
             for d in range(D):
-                name = f"prod{c}_{v0}_{d}"
-                prod = keep.tile([P, width], F32, name=name, tag=f"ring{len(issued) % 6}", align_bytes=64)
-                issued.append(name)
+                prod = product_tile(d, [P, width], f"prod{c}_{v0}_{d}")
                 nc.vector.tensor_tensor(
                     prod[:],
                     h[c][:].indirect(lists[d][:, v0 // 16 : (v0 + width) // 16]),
                     gates[d][:, v0 : v0 + width],
                     MULT,
                 )
-                for b in blocks:
+                for b in banks:
                     nc.tensor.matmul(
                         zt[b][:, cols], prod[:, b * P - v0 : (b + 1) * P - v0], ident[:],
                         start=(d == 0), stop=(d == D - 1), is_transpose=True,
                     )
                 if d == D - 2:
-                    for b in blocks:
+                    for b in banks:
                         nc.tensor.matmul(
                             zt[b][:, cols], neg_h[c][:, b * P : (b + 1) * P], ident[:],
                             start=False, stop=False, is_transpose=True,
                         )
 
+        def in_ring(slots):
+            return lambda d, shape, name: ring_tile(shape, F32, name, slots[d] % RING)
+
+        def in_late(base):
+            return lambda d, shape, name: late.tile(
+                shape, F32, name=name, align_bytes=64, offset=base + d * 4 * QUARTER
+            )
+
         def round_z(c0, count, v0, width):
+            rows = slice(c0 * P // PACK, (c0 + count) * P // PACK)
             for b in range(v0 // P, (v0 + width) // P):
                 nc.scalar.activation(
-                    out=zt_bf[b][:].rearrange("v (u p e) -> v u p e", u=2, e=2)[:, :, 32 * c0 : 32 * (c0 + count), :],
-                    in_=zt[b][:, c0 * P : (c0 + count) * P].rearrange("v (q u e) -> v u q e", u=2, e=2),
+                    out=zt_bf[b][:].rearrange("v (u p e) -> v u p e", u=2, e=2)[:, :, rows, :],
+                    in_=zt[b][:, c0 * P : (c0 + count) * P].rearrange("v (p u e) -> v u p e", u=2, e=2),
                     func=COPY,
                     scale=-1.0,
                 )
 
-        def finish(v0, width, copy_out):
-            nb = width // P
-            turned = psum.tile([P, nb, 2, P], F32, name=f"turned{v0}", tag="turned", bufs=2)
-            for b in range(nb):
+        def finish(v0, width, z_bf, z_codes, z_scales, copy_out):
+            count = width // P
+            turned = psum.tile([P, count, 2, P], F32, name=f"turned{v0}", tag="turned", bufs=2)
+            for b in range(count):
                 words = zt_bf[v0 // P + b][:].bitcast(F32)
                 for u in range(2):
                     nc.tensor.transpose(turned[:, b, u, :], words[:, u * P : (u + 1) * P], ident[:])
-            z_bf = keep.tile([P, width * PACK], BF16, name=f"z_bf{v0}", align_bytes=64)
             nc.scalar.copy(
-                out=z_bf[:].bitcast(F32).rearrange("p (b v u) -> p b v u", b=nb, u=2),
+                out=z_bf[:].bitcast(F32).rearrange("p (b v u) -> p b v u", b=count, u=2),
                 in_=turned[:].rearrange("p b u v -> p b v u"),
             )
-            z_codes = keep.tile([P, width], U32, name=f"z_codes{v0}", align_bytes=64)
-            z_scales = keep.tile([P, width], U8, name=f"z_scales{v0}", align_bytes=64)
             nc.vector.quantize_mx(out=z_codes[:].bitcast(FP8X4), scales=z_scales[:], in_=z_bf[:])
-            result = keep.tile([P, 2, width], F32, name=f"result{v0}", align_bytes=256)
+            result = keep.tile([P, N // P, width], F32, name=f"result{v0}", align_bytes=256)
             for m in range(N // P):
                 acc = psum.tile([P, width], F32, name=f"out_acc{v0}_{m}", tag="acc", bufs=2)
                 nc.tensor.matmul_mx(
@@ -193,35 +209,55 @@ def tile_picked_wlapl_gelu_l_kernel(
                 out=out.rearrange("(m p) v -> p m v", p=P)[:, :, v0 : v0 + width], in_=result[:]
             )
 
+        def z_tiles(v0):
+            return (
+                keep.tile([P, QUARTER * PACK], BF16, name=f"z_bf{v0}", align_bytes=64),
+                keep.tile([P, QUARTER], U32, name=f"z_codes{v0}", align_bytes=64),
+                keep.tile([P, QUARTER], U8, name=f"z_scales{v0}", align_bytes=64),
+            )
+
+        on_scalar, on_vector = nc.scalar.copy, nc.vector.tensor_copy
+
         project(0)
         project(1)
         negate(0)
-        load_w1(2, 1)
-        load_w1(3, 1)
+        for c in (2, 3):
+            for g in range(PASSES):
+                load_w1(c, g)
         nc.sync.dma_start(out=w2_codes[:].bitcast(I32), in_=w2_words[0].bitcast(I32))
         w2_scale_rows = w2_scales[0].bitcast(I32).rearrange("(q r) w -> r q w", r=4)
         for r in range(4):
             nc.sync.dma_start(out=w2_plane[:].bitcast(I32)[r:P:32], in_=w2_scale_rows[r])
-        neighbours(0, 0, T)
+
+        neighbours(0, 0, T, in_ring(range(0, 4)))
         project(2)
         negate(1)
         project(3)
         negate(2)
         negate(3)
-        neighbours(1, 0, T)
+        neighbours(1, 0, T, in_ring(range(4, 8)))
         round_z(0, 2, 0, T)
-        half, quarter = T // 2, T // 4
-        for v0 in (0, half):
-            neighbours(2, v0, half)
-            round_z(2, 1, v0, half)
-            if v0 == 0:
-                pieces = ((0, half, (nc.scalar.copy, nc.scalar.copy)),)
-            else:
-                pieces = (
-                    (half, quarter, (nc.vector.tensor_copy, nc.vector.tensor_copy)),
-                    (half + quarter, quarter, (nc.scalar.copy, nc.vector.tensor_copy)),
-                )
-            for v1, width, copy_out in pieces:
-                neighbours(3, v1, width)
-                round_z(3, 1, v1, width)
-                finish(v1, width, copy_out)
+
+        neighbours(2, 0, HALF, in_ring(range(8, 12)))
+        round_z(2, 1, 0, HALF)
+        neighbours(3, 0, HALF, in_ring(range(12, 16)))
+        round_z(3, 1, 0, HALF)
+        third, fourth = 0, D * 4 * QUARTER
+        finish(
+            0,
+            HALF,
+            late.tile([P, HALF * PACK], BF16, name="z_bf0", align_bytes=64, offset=third),
+            late.tile([P, HALF], U32, name="z_codes0", align_bytes=64, offset=fourth + 2 * QUARTER),
+            late.tile([P, HALF], U8, name="z_scales0", align_bytes=64, offset=fourth + 3 * 4 * QUARTER),
+            (on_scalar, on_scalar),
+        )
+
+        neighbours(2, HALF, HALF, in_ring((12, 15, 13, 14)))
+        round_z(2, 1, HALF, HALF)
+        for v0, base, copy_out in (
+            (HALF, third, (on_vector, on_vector)),
+            (HALF + QUARTER, fourth, (on_scalar, on_vector)),
+        ):
+            neighbours(3, v0, QUARTER, in_late(base))
+            round_z(3, 1, v0, QUARTER)
+            finish(v0, QUARTER, *z_tiles(v0), copy_out)

@@ -17,6 +17,7 @@ FP8X4 = mybir.dt.float8_e4m3fn_x4
 FP4X4 = mybir.dt.float4_e2m1fn_x4
 GELU = mybir.ActivationFunctionType.Gelu_apprx_tanh
 COPY = mybir.ActivationFunctionType.Copy
+IDENTITY = mybir.ActivationFunctionType.Identity
 MULT = mybir.AluOpType.mult
 
 P = 128
@@ -25,7 +26,8 @@ PASSES = K // (P * PACK)
 BLOCKS = H // P
 HALF, QUARTER = T // 2, T // 4
 SPARE = 8
-RING = 7
+AFTER_ROUND, AFTER_QUANTISE = 5, 10
+RAW = 4 * PACK * P
 
 
 def tile_picked_wlapl_gelu_l_kernel(
@@ -34,39 +36,41 @@ def tile_picked_wlapl_gelu_l_kernel(
     nc = tc.nc
     with ExitStack() as ctx:
         keep = ctx.enter_context(tc.tile_pool(name="keep", bufs=1))
+        early = ctx.enter_context(tc.tile_pool(name="early", bufs=1))
         late = ctx.enter_context(tc.tile_pool(name="late", bufs=1))
         psum = ctx.enter_context(tc.psum_pool(name="psum", bufs=1))
 
-        def ring_tile(shape, dtype, name, slot):
-            return keep.tile(shape, dtype, name=name, tag=f"ring{slot}", align_bytes=64)
-
         lists = [keep.tile([P, T // 16], U16, name=f"list{d}") for d in range(D)]
-        gates = [keep.tile([P, T], F32, name=f"gate{d}", align_bytes=256) for d in range(D)]
-        x_codes = [keep.tile([P, T], U32, name=f"x_codes{g}", align_bytes=256) for g in range(PASSES)]
+        gates = [keep.tile([P, T], F32, name=f"gate{d}", tag=f"gate{d}", align_bytes=256) for d in range(D)]
+        x_first = keep.tile([P, T], U32, align_bytes=256)
+        x_second = [keep.tile([P, HALF], U32, name=f"x_second{s}", align_bytes=256) for s in range(2)]
+        x_codes = [[x_first[:, :HALF], x_first[:, HALF:]], [x_second[0][:], x_second[1][:]]]
         x_planes = keep.tile([P, PASSES * T], U8, align_bytes=256)
         w2_codes = keep.tile([P, 2 * N], U8, align_bytes=64)
         w2_plane = keep.tile([P, N], U8, align_bytes=64)
         ident = keep.tile([P, P], F32)
         h = [keep.tile([P, T + SPARE if c < 2 else T], F32, name=f"h{c}") for c in range(BLOCKS)]
         neg_h = [keep.tile([P, T], F32, name=f"neg_h{c}") for c in range(BLOCKS)]
-        zt = [psum.tile([P, H], F32, name=f"zt{b}") for b in range(T // P)]
+        zt = [psum.tile([P, H], F32, name=f"zt{b}", tag=f"zt{b}") for b in range(T // P)]
         zt_bf = [keep.tile([P, H], BF16, name=f"zt_bf{b}") for b in range(T // P)]
 
-        grouped_slot = {1: 2, 2: 6, 3: 0}
-        codes_slot = {1: 3}
-        bias = {c: ring_tile([P, 1], F32, f"bias{c}", grouped_slot[c + 1]) for c in range(2)}
+        bias = {c: keep.tile([P, 1], F32, name=f"bias{c}", tag=f"w1_bf{c + 1}", align_bytes=64) for c in range(2)}
+        round_bias = late.tile([P, (AFTER_QUANTISE - AFTER_ROUND) * QUARTER], F32, align_bytes=64, offset=0)
 
         nc.gpsimd.memset(x_planes[:].bitcast(I32), 0)
         nc.vector.memset(w2_plane[:].bitcast(I32), 0)
         for c in bias:
             nc.vector.memset(bias[c][:], 0.0)
+        nc.vector.memset(round_bias[:, :1], 0.0)
         make_identity(nc, ident[:])
 
         w1_rows = w1.rearrange("(g p j) i -> g p j i", p=P, j=PACK)
         w1_raw = {}
 
         def load_w1(c, g):
-            raw = keep.tile([P, PACK, P], F32, name=f"w1_raw{c}_{g}", tag=f"w1_raw{c % 2}_{g}", align_bytes=256)
+            raw = early.tile(
+                [P, PACK, P], F32, name=f"w1_raw{c}_{g}", align_bytes=256, offset=(3 * c + g) * RAW
+            )
             nc.sync.dma_start(out=raw[:], in_=w1_rows[g][:, :, c * P : (c + 1) * P])
             w1_raw[(c, g)] = raw
 
@@ -80,29 +84,30 @@ def tile_picked_wlapl_gelu_l_kernel(
         for r in range(4):
             nc.sync.dma_start(out=x_plane_words[r:P:32], in_=x_scale_rows[r])
         load_w1(0, 1)
-        for g in range(PASSES):
-            nc.sync.dma_start(
-                out=x_codes[g][:].bitcast(I32), in_=x_words[g].rearrange("p n t -> p (n t)").bitcast(I32)
-            )
+        x_rows = [x_words[g].rearrange("p n t -> p (n t)").bitcast(I32) for g in range(PASSES)]
+        nc.sync.dma_start(out=x_first[:].bitcast(I32), in_=x_rows[0])
+        for s in range(2):
+            nc.sync.dma_start(out=x_second[s][:].bitcast(I32), in_=x_rows[1][:, s * HALF : (s + 1) * HALF])
         load_neighbours(0)
         for g in range(PASSES):
             load_w1(1, g)
         for d in range(1, D):
             load_neighbours(d)
+        for c in (2, 3):
+            for g in range(PASSES):
+                load_w1(c, g)
+        nc.sync.dma_start(out=w2_codes[:].bitcast(I32), in_=w2_words[0].bitcast(I32))
+        w2_scale_rows = w2_scales[0].bitcast(I32).rearrange("(q r) w -> r q w", r=4)
+        for r in range(4):
+            nc.sync.dma_start(out=w2_plane[:].bitcast(I32)[r:P:32], in_=w2_scale_rows[r])
 
         for c in range(2):
             nc.scalar.activation(out=h[c][:, T:], in_=ident[:, :SPARE], func=GELU)
 
         def project(c):
             width = P * PACK
-            if c in grouped_slot:
-                grouped = ring_tile([P, PASSES * width], BF16, f"w1_bf{c}", grouped_slot[c])
-            else:
-                grouped = keep.tile([P, PASSES * width], BF16, name=f"w1_bf{c}", align_bytes=64)
-            if c in codes_slot:
-                codes = ring_tile([P, PASSES * P], U32, f"w1_codes{c}", codes_slot[c])
-            else:
-                codes = keep.tile([P, PASSES * P], U32, name=f"w1_codes{c}", align_bytes=64)
+            grouped = keep.tile([P, PASSES * width], BF16, name=f"w1_bf{c}", tag=f"w1_bf{c}", align_bytes=64)
+            codes = keep.tile([P, PASSES * P], U32, name=f"w1_codes{c}", align_bytes=64)
             scales = keep.tile([P, PASSES * P], U8, name=f"w1_scales{c}", align_bytes=64)
             first = c == 0
             cast = nc.vector.tensor_copy if first else nc.scalar.copy
@@ -126,7 +131,7 @@ def tile_picked_wlapl_gelu_l_kernel(
                         out=pre[s][:],
                         lhsT=codes[:, cols].bitcast(FP8X4),
                         lhsT_scale=scales[:, cols],
-                        rhs=x_codes[g][:, halves[s]].bitcast(FP8X4),
+                        rhs=x_codes[g][s].bitcast(FP8X4),
                         rhs_scale=x_planes[:, g * T : (g + 1) * T][:, halves[s]],
                         start=(g == 0),
                         stop=(g == PASSES - 1),
@@ -139,9 +144,13 @@ def tile_picked_wlapl_gelu_l_kernel(
         def negate(c):
             nc.scalar.activation(out=neg_h[c][:], in_=h[c][:, :T], func=COPY, scale=-1.0)
 
-        def neighbours(c, v0, width, product_tile):
+        def neighbours(c, v0, width, product_tile, sums=None):
             banks = range(v0 // P, (v0 + width) // P)
-            cols = slice(c * P, (c + 1) * P)
+            sums = sums or {b: zt[b][:, c * P : (c + 1) * P] for b in banks}
+            for b in banks:
+                nc.tensor.matmul(
+                    sums[b], neg_h[c][:, b * P : (b + 1) * P], ident[:], start=True, stop=False, is_transpose=True
+                )
             for d in range(D):
                 prod = product_tile(d, [P, width], f"prod{c}_{v0}_{d}")
                 nc.vector.tensor_tensor(
@@ -152,35 +161,31 @@ def tile_picked_wlapl_gelu_l_kernel(
                 )
                 for b in banks:
                     nc.tensor.matmul(
-                        zt[b][:, cols], prod[:, b * P - v0 : (b + 1) * P - v0], ident[:],
-                        start=(d == 0), stop=(d == D - 1), is_transpose=True,
+                        sums[b], prod[:, b * P - v0 : (b + 1) * P - v0], ident[:],
+                        start=False, stop=(d == D - 1), is_transpose=True,
                     )
-                if d == D - 2:
-                    for b in banks:
-                        nc.tensor.matmul(
-                            zt[b][:, cols], neg_h[c][:, b * P : (b + 1) * P], ident[:],
-                            start=False, stop=False, is_transpose=True,
-                        )
 
-        def in_ring(slots):
-            return lambda d, shape, name: ring_tile(shape, F32, name, slots[d] % RING)
-
-        def in_late(base):
-            return lambda d, shape, name: late.tile(
-                shape, F32, name=name, align_bytes=64, offset=base + d * 4 * QUARTER
+        def placed(pool, offsets):
+            return lambda d, shape, name: (
+                pool.tile(shape, F32, name=name, align_bytes=256 if pool is early else 64, offset=offsets[d])
+                if d in offsets
+                else keep.tile(shape, F32, name=name, align_bytes=64)
             )
 
-        def round_z(c0, count, v0, width):
+        def round_z(c0, count, v0, width, sums=None, zero=None):
             rows = slice(c0 * P // PACK, (c0 + count) * P // PACK)
             for b in range(v0 // P, (v0 + width) // P):
                 nc.scalar.activation(
                     out=zt_bf[b][:].rearrange("v (u p e) -> v u p e", u=2, e=2)[:, :, rows, :],
-                    in_=zt[b][:, c0 * P : (c0 + count) * P].rearrange("v (p u e) -> v u p e", u=2, e=2),
-                    func=COPY,
+                    in_=(sums[b] if sums else zt[b][:, c0 * P : (c0 + count) * P]).rearrange(
+                        "v (p u e) -> v u p e", u=2, e=2
+                    ),
+                    func=IDENTITY if zero is not None else COPY,
+                    bias=zero if zero is not None else 0.0,
                     scale=-1.0,
                 )
 
-        def finish(v0, width, z_bf, z_codes, z_scales, copy_out):
+        def turn_back(v0, width, z_bf):
             count = width // P
             turned = psum.tile([P, count, 2, P], F32, name=f"turned{v0}", tag="turned", bufs=2)
             for b in range(count):
@@ -188,11 +193,13 @@ def tile_picked_wlapl_gelu_l_kernel(
                 for u in range(2):
                     nc.tensor.transpose(turned[:, b, u, :], words[:, u * P : (u + 1) * P], ident[:])
             nc.scalar.copy(
-                out=z_bf[:].bitcast(F32).rearrange("p (b v u) -> p b v u", b=count, u=2),
+                out=z_bf.bitcast(F32).rearrange("p (b v u) -> p b v u", b=count, u=2),
                 in_=turned[:].rearrange("p b u v -> p b v u"),
             )
-            nc.vector.quantize_mx(out=z_codes[:].bitcast(FP8X4), scales=z_scales[:], in_=z_bf[:])
-            result = keep.tile([P, N // P, width], F32, name=f"result{v0}", align_bytes=256)
+
+        def finish(v0, width, z_bf, z_codes, copy_out):
+            z_scales = keep.tile([P, width], U8, name=f"z_scales{v0}", align_bytes=64)
+            nc.vector.quantize_mx(out=z_codes[:].bitcast(FP8X4), scales=z_scales[:], in_=z_bf)
             for m in range(N // P):
                 acc = psum.tile([P, width], F32, name=f"out_acc{v0}_{m}", tag="acc", bufs=2)
                 nc.tensor.matmul_mx(
@@ -204,60 +211,55 @@ def tile_picked_wlapl_gelu_l_kernel(
                     start=True,
                     stop=True,
                 )
-                copy_out[m](out=result[:, m, :], in_=acc[:])
-            nc.sync.dma_start(
-                out=out.rearrange("(m p) v -> p m v", p=P)[:, :, v0 : v0 + width], in_=result[:]
-            )
-
-        def z_tiles(v0):
-            return (
-                keep.tile([P, QUARTER * PACK], BF16, name=f"z_bf{v0}", align_bytes=64),
-                keep.tile([P, QUARTER], U32, name=f"z_codes{v0}", align_bytes=64),
-                keep.tile([P, QUARTER], U8, name=f"z_scales{v0}", align_bytes=64),
-            )
+                result = keep.tile([P, width], F32, name=f"result{v0}_{m}", align_bytes=256)
+                copy_out[m](out=result[:], in_=acc[:])
+                nc.sync.dma_start(out=out[m * P : (m + 1) * P, v0 : v0 + width], in_=result[:])
 
         on_scalar, on_vector = nc.scalar.copy, nc.vector.tensor_copy
 
         project(0)
-        project(1)
         negate(0)
-        for c in (2, 3):
-            for g in range(PASSES):
-                load_w1(c, g)
-        nc.sync.dma_start(out=w2_codes[:].bitcast(I32), in_=w2_words[0].bitcast(I32))
-        w2_scale_rows = w2_scales[0].bitcast(I32).rearrange("(q r) w -> r q w", r=4)
-        for r in range(4):
-            nc.sync.dma_start(out=w2_plane[:].bitcast(I32)[r:P:32], in_=w2_scale_rows[r])
-
-        neighbours(0, 0, T, in_ring(range(0, 4)))
-        project(2)
+        project(1)
+        neighbours(0, 0, T, placed(early, {2: 4 * RAW - RAW // 2, 3: 4 * RAW + RAW // 2}))
         negate(1)
+        project(2)
         project(3)
         negate(2)
         negate(3)
-        neighbours(1, 0, T, in_ring(range(4, 8)))
+        neighbours(1, 0, T, placed(early, {2: 7 * RAW, 3: 10 * RAW}))
         round_z(0, 2, 0, T)
 
-        neighbours(2, 0, HALF, in_ring(range(8, 12)))
+        neighbours(2, 0, HALF, placed(late, {}))
         round_z(2, 1, 0, HALF)
-        neighbours(3, 0, HALF, in_ring(range(12, 16)))
-        round_z(3, 1, 0, HALF)
-        third, fourth = 0, D * 4 * QUARTER
-        finish(
-            0,
-            HALF,
-            late.tile([P, HALF * PACK], BF16, name="z_bf0", align_bytes=64, offset=third),
-            late.tile([P, HALF], U32, name="z_codes0", align_bytes=64, offset=fourth + 2 * QUARTER),
-            late.tile([P, HALF], U8, name="z_scales0", align_bytes=64, offset=fourth + 3 * 4 * QUARTER),
-            (on_scalar, on_scalar),
+        neighbours(3, 0, HALF, placed(late, {}))
+        round_z(3, 1, 0, HALF, zero=round_bias[:, :1])
+        held = lambda first: placed(
+            late, {d: (first + d - AFTER_ROUND) * 4 * QUARTER for d in range(D) if first + d >= AFTER_ROUND}
         )
+        z_half = late.tile(
+            [P, (4 * D - AFTER_QUANTISE) * 2 * QUARTER], BF16, align_bytes=64,
+            offset=(AFTER_QUANTISE - AFTER_ROUND) * 4 * QUARTER,
+        )
+        turn_back(0, HALF, z_half[:, : HALF * PACK])
+        codes_half = keep.tile([P, HALF], U32, align_bytes=64)
+        finish(0, HALF, z_half[:, : HALF * PACK], codes_half, (on_scalar, on_scalar))
 
-        neighbours(2, HALF, HALF, in_ring((12, 15, 13, 14)))
-        round_z(2, 1, HALF, HALF)
-        for v0, base, copy_out in (
-            (HALF, third, (on_vector, on_vector)),
-            (HALF + QUARTER, fourth, (on_scalar, on_vector)),
-        ):
-            neighbours(3, v0, QUARTER, in_late(base))
-            round_z(3, 1, v0, QUARTER)
-            finish(v0, QUARTER, *z_tiles(v0), copy_out)
+        third, fourth = HALF, HALF + QUARTER
+        neighbours(2, third, QUARTER, held(0))
+        neighbours(3, third, QUARTER, held(D))
+        round_z(2, 2, third, QUARTER)
+        z_third = keep.tile([P, QUARTER * PACK], BF16, align_bytes=64)
+        turn_back(third, QUARTER, z_third[:])
+
+        neighbours(2, fourth, QUARTER, held(2 * D))
+        round_z(2, 1, fourth, QUARTER)
+        last_sums = psum.tile([P, P], F32, tag="zt0")
+        sums = {fourth // P: last_sums[:]}
+        neighbours(3, fourth, QUARTER, held(3 * D), sums)
+        codes_third = keep.tile([P, QUARTER], U32, tag=f"gate{D - 2}", align_bytes=256)
+        finish(third, QUARTER, z_third[:], codes_third, (on_vector, on_vector))
+        round_z(3, 1, fourth, QUARTER, sums)
+        z_fourth = keep.tile([P, QUARTER * PACK], BF16, align_bytes=64)
+        turn_back(fourth, QUARTER, z_fourth[:])
+        codes_fourth = keep.tile([P, QUARTER], U32, align_bytes=64)
+        finish(fourth, QUARTER, z_fourth[:], codes_fourth, (on_scalar, on_vector))

@@ -26,7 +26,7 @@ PASSES = K // (P * PACK)
 BLOCKS = H // P
 HALF, QUARTER = T // 2, T // 4
 SPARE = 8
-AFTER_ROUND, AFTER_QUANTISE = 5, 10
+AFTER_ROUND, AFTER_QUANTISE = 5, 11
 RAW = 4 * PACK * P
 
 
@@ -42,9 +42,7 @@ def tile_picked_wlapl_gelu_l_kernel(
 
         lists = [keep.tile([P, T // 16], U16, name=f"list{d}") for d in range(D)]
         gates = [keep.tile([P, T], F32, name=f"gate{d}", tag=f"gate{d}", align_bytes=256) for d in range(D)]
-        x_first = keep.tile([P, T], U32, align_bytes=256)
-        x_second = [keep.tile([P, HALF], U32, name=f"x_second{s}", align_bytes=256) for s in range(2)]
-        x_codes = [[x_first[:, :HALF], x_first[:, HALF:]], [x_second[0][:], x_second[1][:]]]
+        x_codes = [keep.tile([P, T], U32, name=f"x_codes{g}", align_bytes=256) for g in range(PASSES)]
         x_planes = keep.tile([P, PASSES * T], U8, align_bytes=256)
         w2_codes = keep.tile([P, 2 * N], U8, align_bytes=64)
         w2_plane = keep.tile([P, N], U8, align_bytes=64)
@@ -55,12 +53,14 @@ def tile_picked_wlapl_gelu_l_kernel(
         zt_bf = [keep.tile([P, H], BF16, name=f"zt_bf{b}") for b in range(T // P)]
 
         bias = {c: keep.tile([P, 1], F32, name=f"bias{c}", tag=f"w1_bf{c + 1}", align_bytes=64) for c in range(2)}
-        round_bias = late.tile([P, (AFTER_QUANTISE - AFTER_ROUND) * QUARTER], F32, align_bytes=64, offset=0)
+        round_bias = late.tile([P, (AFTER_QUANTISE - AFTER_ROUND) * QUARTER], F32, align_bytes=64,
+                               offset=AFTER_ROUND * 4 * QUARTER)
+        bias[3] = late.tile([P, AFTER_ROUND * QUARTER], F32, name="bias3", align_bytes=64, offset=0)
 
         nc.gpsimd.memset(x_planes[:].bitcast(I32), 0)
         nc.vector.memset(w2_plane[:].bitcast(I32), 0)
         for c in bias:
-            nc.vector.memset(bias[c][:], 0.0)
+            nc.vector.memset(bias[c][:, :1], 0.0)
         nc.vector.memset(round_bias[:, :1], 0.0)
         make_identity(nc, ident[:])
 
@@ -75,23 +75,24 @@ def tile_picked_wlapl_gelu_l_kernel(
             w1_raw[(c, g)] = raw
 
         def load_neighbours(d):
-            nc.sync.dma_start(lists[d][:], (pos1, pos2, pos3, pos4)[d])
             nc.sync.dma_start(out=gates[d][:], in_=gate[d])
+            nc.sync.dma_start(lists[d][:], (pos1, pos2, pos3, pos4)[d])
 
         load_w1(0, 0)
+        load_w1(0, 1)
         x_plane_words = x_planes[:].bitcast(I32).rearrange("p (g w) -> p g w", g=PASSES)
         x_scale_rows = x_scales.bitcast(I32).rearrange("g (q r) w -> r q g w", r=4)
         for r in range(4):
             nc.sync.dma_start(out=x_plane_words[r:P:32], in_=x_scale_rows[r])
-        load_w1(0, 1)
-        x_rows = [x_words[g].rearrange("p n t -> p (n t)").bitcast(I32) for g in range(PASSES)]
-        nc.sync.dma_start(out=x_first[:].bitcast(I32), in_=x_rows[0])
-        for s in range(2):
-            nc.sync.dma_start(out=x_second[s][:].bitcast(I32), in_=x_rows[1][:, s * HALF : (s + 1) * HALF])
-        load_neighbours(0)
         for g in range(PASSES):
-            load_w1(1, g)
-        for d in range(1, D):
+            nc.sync.dma_start(
+                out=x_codes[g][:].bitcast(I32), in_=x_words[g].rearrange("p n t -> p (n t)").bitcast(I32)
+            )
+        load_neighbours(0)
+        load_w1(1, 0)
+        load_neighbours(1)
+        load_w1(1, 1)
+        for d in range(2, D):
             load_neighbours(d)
         for c in (2, 3):
             for g in range(PASSES):
@@ -131,14 +132,14 @@ def tile_picked_wlapl_gelu_l_kernel(
                         out=pre[s][:],
                         lhsT=codes[:, cols].bitcast(FP8X4),
                         lhsT_scale=scales[:, cols],
-                        rhs=x_codes[g][s].bitcast(FP8X4),
+                        rhs=x_codes[g][:, halves[s]].bitcast(FP8X4),
                         rhs_scale=x_planes[:, g * T : (g + 1) * T][:, halves[s]],
                         start=(g == 0),
                         stop=(g == PASSES - 1),
                     )
             for s in range(2):
                 nc.scalar.activation(
-                    out=h[c][:, halves[s]], in_=pre[s][:], func=GELU, bias=bias[c][:] if c in bias else 0.0
+                    out=h[c][:, halves[s]], in_=pre[s][:], func=GELU, bias=bias[c][:, :1] if c in bias else 0.0
                 )
 
         def negate(c):
@@ -185,21 +186,24 @@ def tile_picked_wlapl_gelu_l_kernel(
                     scale=-1.0,
                 )
 
-        def turn_back(v0, width, z_bf):
-            count = width // P
-            turned = psum.tile([P, count, 2, P], F32, name=f"turned{v0}", tag="turned", bufs=2)
-            for b in range(count):
+        def turn_back(v0, z_bf, tag):
+            turned = psum.tile([P, len(z_bf), 2, P], F32, name=f"turned{v0}", tag=tag)
+            for b in range(len(z_bf)):
                 words = zt_bf[v0 // P + b][:].bitcast(F32)
                 for u in range(2):
                     nc.tensor.transpose(turned[:, b, u, :], words[:, u * P : (u + 1) * P], ident[:])
-            nc.scalar.copy(
-                out=z_bf.bitcast(F32).rearrange("p (b v u) -> p b v u", b=count, u=2),
-                in_=turned[:].rearrange("p b u v -> p b v u"),
-            )
+            for b in range(len(z_bf)):
+                nc.scalar.copy(
+                    out=z_bf[b].bitcast(F32).rearrange("p (v u) -> p v u", u=2),
+                    in_=turned[:, b].rearrange("p u v -> p v u"),
+                )
 
-        def finish(v0, width, z_bf, z_codes, copy_out):
+        def finish(v0, z_bf, z_codes, copy_out):
+            width = len(z_bf) * P
             z_scales = keep.tile([P, width], U8, name=f"z_scales{v0}", align_bytes=64)
-            nc.vector.quantize_mx(out=z_codes[:].bitcast(FP8X4), scales=z_scales[:], in_=z_bf)
+            for b in range(len(z_bf)):
+                cols = slice(b * P, (b + 1) * P)
+                nc.vector.quantize_mx(out=z_codes[:, cols].bitcast(FP8X4), scales=z_scales[:, cols], in_=z_bf[b])
             for m in range(N // P):
                 acc = psum.tile([P, width], F32, name=f"out_acc{v0}_{m}", tag="acc", bufs=2)
                 nc.tensor.matmul_mx(
@@ -229,37 +233,38 @@ def tile_picked_wlapl_gelu_l_kernel(
         neighbours(1, 0, T, placed(early, {2: 7 * RAW, 3: 10 * RAW}))
         round_z(0, 2, 0, T)
 
-        neighbours(2, 0, HALF, placed(late, {}))
-        round_z(2, 1, 0, HALF)
-        neighbours(3, 0, HALF, placed(late, {}))
-        round_z(3, 1, 0, HALF, zero=round_bias[:, :1])
-        held = lambda first: placed(
-            late, {d: (first + d - AFTER_ROUND) * 4 * QUARTER for d in range(D) if first + d >= AFTER_ROUND}
-        )
-        z_half = late.tile(
+        half_sums = [psum.tile([P, 2 * P], F32, name=f"half_sums{b}", tag=f"spare{b}") for b in range(2)]
+        for c in (2, 3):
+            sums = {b: half_sums[b][:, (c - 2) * P : (c - 1) * P] for b in range(2)}
+            neighbours(c, 0, HALF, placed(late, {}), sums)
+        round_z(2, 2, 0, HALF, {b: half_sums[b][:] for b in range(2)}, zero=round_bias[:, :1])
+        held = lambda first: placed(late, {d: (first + d) * 4 * QUARTER for d in range(D)})
+        z_held = late.tile(
             [P, (4 * D - AFTER_QUANTISE) * 2 * QUARTER], BF16, align_bytes=64,
-            offset=(AFTER_QUANTISE - AFTER_ROUND) * 4 * QUARTER,
+            offset=AFTER_QUANTISE * 4 * QUARTER,
         )
-        turn_back(0, HALF, z_half[:, : HALF * PACK])
+        z_second = keep.tile([P, QUARTER * PACK], BF16, align_bytes=64)
+        z_half = [z_held[:, : QUARTER * PACK], z_second[:]]
+        turn_back(0, z_half, "zt0")
         codes_half = keep.tile([P, HALF], U32, align_bytes=64)
-        finish(0, HALF, z_half[:, : HALF * PACK], codes_half, (on_scalar, on_scalar))
+        finish(0, z_half, codes_half, (on_scalar, on_scalar))
 
         third, fourth = HALF, HALF + QUARTER
         neighbours(2, third, QUARTER, held(0))
         neighbours(3, third, QUARTER, held(D))
         round_z(2, 2, third, QUARTER)
         z_third = keep.tile([P, QUARTER * PACK], BF16, align_bytes=64)
-        turn_back(third, QUARTER, z_third[:])
+        turn_back(third, [z_third[:]], "spare0")
 
         neighbours(2, fourth, QUARTER, held(2 * D))
         round_z(2, 1, fourth, QUARTER)
-        last_sums = psum.tile([P, P], F32, tag="zt0")
+        last_sums = psum.tile([P, P], F32, tag="zt1")
         sums = {fourth // P: last_sums[:]}
         neighbours(3, fourth, QUARTER, held(3 * D), sums)
         codes_third = keep.tile([P, QUARTER], U32, tag=f"gate{D - 2}", align_bytes=256)
-        finish(third, QUARTER, z_third[:], codes_third, (on_vector, on_vector))
+        finish(third, [z_third[:]], codes_third, (on_vector, on_vector))
         round_z(3, 1, fourth, QUARTER, sums)
         z_fourth = keep.tile([P, QUARTER * PACK], BF16, align_bytes=64)
-        turn_back(fourth, QUARTER, z_fourth[:])
+        turn_back(fourth, [z_fourth[:]], "spare1")
         codes_fourth = keep.tile([P, QUARTER], U32, align_bytes=64)
-        finish(fourth, QUARTER, z_fourth[:], codes_fourth, (on_scalar, on_vector))
+        finish(fourth, [z_fourth[:]], codes_fourth, (on_scalar, on_vector))

@@ -48,7 +48,7 @@ def tile_picked_wlapl_gelu_l_kernel(
         w2_plane = keep.tile([P, N], U8, align_bytes=64)
         ident = keep.tile([P, P], F32)
         h = [keep.tile([P, T + SPARE if c < 2 else T], F32, name=f"h{c}") for c in range(BLOCKS)]
-        neg_h = [keep.tile([P, T], F32, name=f"neg_h{c}") for c in range(BLOCKS)]
+        neg_h = {}
         zt = [psum.tile([P, H], F32, name=f"zt{b}", tag=f"zt{b}") for b in range(T // P)]
         zt_bf = [keep.tile([P, H], BF16, name=f"zt_bf{b}") for b in range(T // P)]
 
@@ -66,12 +66,15 @@ def tile_picked_wlapl_gelu_l_kernel(
 
         w1_rows = w1.rearrange("(g p j) i -> g p j i", p=P, j=PACK)
         w1_raw = {}
+        raw_place = {
+            (0, 0): (0, 1), (0, 1): (RAW, 1), (1, 0): (2 * RAW, 1), (1, 1): (3 * RAW + RAW // 2, 2),
+            (2, 0): (6 * RAW, 1), (2, 1): (7 * RAW, 2), (3, 0): (9 * RAW, 1), (3, 1): (10 * RAW, 1),
+        }
 
         def load_w1(c, g):
-            raw = early.tile(
-                [P, PACK, P], F32, name=f"w1_raw{c}_{g}", align_bytes=256, offset=(3 * c + g) * RAW
-            )
-            nc.sync.dma_start(out=raw[:], in_=w1_rows[g][:, :, c * P : (c + 1) * P])
+            start, count = raw_place[(c, g)]
+            raw = early.tile([P, count, PACK, P], F32, name=f"w1_raw{c}_{g}", align_bytes=256, offset=start)
+            nc.sync.dma_start(out=raw[:, 0], in_=w1_rows[g][:, :, c * P : (c + 1) * P])
             w1_raw[(c, g)] = raw
 
         def load_neighbours(d):
@@ -116,7 +119,7 @@ def tile_picked_wlapl_gelu_l_kernel(
                 part = grouped[:, g * width : (g + 1) * width]
                 cast(
                     out=part.rearrange("p (a n t) -> p a t n", n=4, t=PACK),
-                    in_=w1_raw[(c, g)][:].rearrange("p t (a n) -> p a t n", n=4),
+                    in_=w1_raw[(c, g)][:, 0].rearrange("p t (a n) -> p a t n", n=4),
                 )
                 if first:
                     cols = slice(g * P, (g + 1) * P)
@@ -142,17 +145,24 @@ def tile_picked_wlapl_gelu_l_kernel(
                     out=h[c][:, halves[s]], in_=pre[s][:], func=GELU, bias=bias[c][:, :1] if c in bias else 0.0
                 )
 
-        def negate(c):
+        def negate(c, offset=None):
+            if offset is None:
+                neg_h[c] = keep.tile([P, T], F32, name=f"neg_h{c}")
+            else:
+                neg_h[c] = early.tile([P, T], F32, name=f"neg_h{c}", align_bytes=256, offset=offset)
             nc.scalar.activation(out=neg_h[c][:], in_=h[c][:, :T], func=COPY, scale=-1.0)
 
         def neighbours(c, v0, width, product_tile, sums=None):
             banks = range(v0 // P, (v0 + width) // P)
             sums = sums or {b: zt[b][:, c * P : (c + 1) * P] for b in banks}
-            for b in banks:
-                nc.tensor.matmul(
-                    sums[b], neg_h[c][:, b * P : (b + 1) * P], ident[:], start=True, stop=False, is_transpose=True
-                )
+            joins = 1 if c < 2 else 0
             for d in range(D):
+                if d == joins:
+                    for b in banks:
+                        nc.tensor.matmul(
+                            sums[b], neg_h[c][:, b * P : (b + 1) * P], ident[:],
+                            start=(d == 0), stop=False, is_transpose=True,
+                        )
                 prod = product_tile(d, [P, width], f"prod{c}_{v0}_{d}")
                 nc.vector.tensor_tensor(
                     prod[:],
@@ -163,7 +173,7 @@ def tile_picked_wlapl_gelu_l_kernel(
                 for b in banks:
                     nc.tensor.matmul(
                         sums[b], prod[:, b * P - v0 : (b + 1) * P - v0], ident[:],
-                        start=False, stop=(d == D - 1), is_transpose=True,
+                        start=(d < joins), stop=(d == D - 1), is_transpose=True,
                     )
 
         def placed(pool, offsets):
@@ -222,11 +232,11 @@ def tile_picked_wlapl_gelu_l_kernel(
         on_scalar, on_vector = nc.scalar.copy, nc.vector.tensor_copy
 
         project(0)
-        negate(0)
         project(1)
-        neighbours(0, 0, T, placed(early, {2: 4 * RAW - RAW // 2, 3: 4 * RAW + RAW // 2}))
-        negate(1)
+        negate(0, 4 * RAW)
+        neighbours(0, 0, T, placed(early, {2: 3 * RAW, 3: 5 * RAW}))
         project(2)
+        negate(1, 8 * RAW)
         project(3)
         negate(2)
         negate(3)

@@ -26,7 +26,7 @@ PASSES = K // (P * PACK)
 BLOCKS = H // P
 HALF, QUARTER = T // 2, T // 4
 SPARE = 8
-AFTER_ROUND, AFTER_QUANTISE = 5, 11
+AFTER_ROUND, AFTER_QUANTISE = 7, 12
 RAW = 4 * PACK * P
 
 
@@ -208,16 +208,19 @@ def tile_picked_wlapl_gelu_l_kernel(
                     in_=turned[:, b].rearrange("p u v -> p v u"),
                 )
 
-        def finish(v0, z_bf, z_codes, copy_out):
+        def finish(v0, z_bf, z_codes, copy_out, bank=None):
             width = len(z_bf) * P
             z_scales = keep.tile([P, width], U8, name=f"z_scales{v0}", align_bytes=64)
             for b in range(len(z_bf)):
                 cols = slice(b * P, (b + 1) * P)
                 nc.vector.quantize_mx(out=z_codes[:, cols].bitcast(FP8X4), scales=z_scales[:, cols], in_=z_bf[b])
             for m in range(N // P):
-                acc = psum.tile([P, width], F32, name=f"out_acc{v0}_{m}", tag="acc", bufs=2)
+                if bank is None:
+                    acc = psum.tile([P, width], F32, name=f"out_acc{v0}_{m}", tag="acc", bufs=2)[:]
+                else:
+                    acc = bank[:, m * width : (m + 1) * width]
                 nc.tensor.matmul_mx(
-                    out=acc[:],
+                    out=acc,
                     lhsT=w2_codes[:, 2 * P * m : 2 * P * (m + 1)].bitcast(FP4X4),
                     lhsT_scale=w2_plane[:, P * m : P * (m + 1)],
                     rhs=z_codes[:].bitcast(FP8X4),
@@ -225,9 +228,16 @@ def tile_picked_wlapl_gelu_l_kernel(
                     start=True,
                     stop=True,
                 )
-                result = keep.tile([P, width], F32, name=f"result{v0}_{m}", align_bytes=256)
-                copy_out[m](out=result[:], in_=acc[:])
-                nc.sync.dma_start(out=out[m * P : (m + 1) * P, v0 : v0 + width], in_=result[:])
+                if bank is None:
+                    result = keep.tile([P, width], F32, name=f"result{v0}_{m}", align_bytes=256)
+                    copy_out[m](out=result[:], in_=acc)
+                    nc.sync.dma_start(out=out[m * P : (m + 1) * P, v0 : v0 + width], in_=result[:])
+            if bank is not None:
+                result = keep.tile([P, N // P, width], F32, name=f"result{v0}", align_bytes=256)
+                copy_out[0](out=result[:].rearrange("p m v -> p (m v)"), in_=bank)
+                nc.sync.dma_start(
+                    out=out.rearrange("(m p) v -> p m v", p=P)[:, :, v0 : v0 + width], in_=result[:]
+                )
 
         on_scalar, on_vector = nc.scalar.copy, nc.vector.tensor_copy
 
@@ -271,10 +281,11 @@ def tile_picked_wlapl_gelu_l_kernel(
         last_sums = psum.tile([P, P], F32, tag="zt1")
         sums = {fourth // P: last_sums[:]}
         neighbours(3, fourth, QUARTER, held(3 * D), sums)
-        codes_third = keep.tile([P, QUARTER], U32, tag=f"gate{D - 2}", align_bytes=256)
-        finish(third, [z_third[:]], codes_third, (on_vector, on_vector))
         round_z(3, 1, fourth, QUARTER, sums)
         z_fourth = keep.tile([P, QUARTER * PACK], BF16, align_bytes=64)
         turn_back(fourth, [z_fourth[:]], "spare1")
+        codes_third = keep.tile([P, QUARTER], U32, tag=f"gate{D - 2}", align_bytes=256)
+        out_third = psum.tile([P, N // P * QUARTER], F32, tag="zt1")
+        finish(third, [z_third[:]], codes_third, (on_scalar,), out_third[:])
         codes_fourth = keep.tile([P, QUARTER], U32, align_bytes=64)
         finish(fourth, [z_fourth[:]], codes_fourth, (on_scalar, on_vector))

@@ -68,7 +68,7 @@ def tile_picked_wlapl_gelu_l_kernel(
         w1_raw = {}
         raw_place = {
             (0, 0): (0, 1), (0, 1): (RAW, 1), (1, 0): (2 * RAW, 1), (1, 1): (3 * RAW + RAW // 2, 2),
-            (2, 0): (6 * RAW, 1), (2, 1): (7 * RAW, 2), (3, 0): (9 * RAW, 1), (3, 1): (10 * RAW, 1),
+            (2, 0): (6 * RAW, 1), (2, 1): (7 * RAW, 1), (3, 0): (8 * RAW, 1), (3, 1): (9 * RAW, 2),
         }
 
         def load_w1(c, g):
@@ -246,11 +246,11 @@ def tile_picked_wlapl_gelu_l_kernel(
         negate(0, 4 * RAW)
         neighbours(0, 0, T, placed(early, {2: 3 * RAW, 3: 5 * RAW}))
         project(2)
-        negate(1, 8 * RAW)
         project(3)
+        negate(1, 10 * RAW)
         negate(2)
         negate(3)
-        neighbours(1, 0, T, placed(early, {2: 7 * RAW, 3: 10 * RAW}))
+        neighbours(1, 0, T, placed(early, {2: 7 * RAW, 3: 9 * RAW}))
         round_z(0, 2, 0, T)
 
         half_sums = [psum.tile([P, 2 * P], F32, name=f"half_sums{b}", tag=f"spare{b}") for b in range(2)]

@@ -26,8 +26,22 @@ PASSES = K // (P * PACK)
 BLOCKS = H // P
 HALF, QUARTER = T // 2, T // 4
 SPARE = 8
-AFTER_ROUND, AFTER_QUANTISE = 7, 12
-RAW = 4 * PACK * P
+AFTER_ROUND = 7
+UNIT = 4 * T
+SMALL = 4 * QUARTER
+
+RAW_PLACE = {
+    (0, 0): (0, 1),
+    (0, 1): (UNIT, 1),
+    (1, 0): (2 * UNIT, 1),
+    (1, 1): (3 * UNIT + UNIT // 2, 2),
+    (2, 0): (6 * UNIT, 1),
+    (2, 1): (7 * UNIT, 1),
+    (3, 0): (8 * UNIT, 1),
+    (3, 1): (9 * UNIT, 2),
+}
+PRODUCT_PLACE = {0: {2: 3 * UNIT, 3: 5 * UNIT}, 1: {2: 7 * UNIT, 3: 9 * UNIT}}
+NEG_PLACE = {0: 4 * UNIT, 1: 10 * UNIT}
 
 
 def tile_picked_wlapl_gelu_l_kernel(
@@ -53,27 +67,24 @@ def tile_picked_wlapl_gelu_l_kernel(
         zt_bf = [keep.tile([P, H], BF16, name=f"zt_bf{b}") for b in range(T // P)]
 
         bias = {c: keep.tile([P, 1], F32, name=f"bias{c}", tag=f"w1_bf{c + 1}", align_bytes=64) for c in range(2)}
-        round_bias = late.tile([P, (AFTER_QUANTISE - AFTER_ROUND) * QUARTER], F32, align_bytes=64,
-                               offset=AFTER_ROUND * 4 * QUARTER)
+        half_bias = late.tile([P, (4 * D - AFTER_ROUND) * QUARTER], F32, align_bytes=64, offset=AFTER_ROUND * SMALL)
         bias[3] = late.tile([P, AFTER_ROUND * QUARTER], F32, name="bias3", align_bytes=64, offset=0)
 
         nc.gpsimd.memset(x_planes[:].bitcast(I32), 0)
         nc.vector.memset(w2_plane[:].bitcast(I32), 0)
         for c in bias:
             nc.vector.memset(bias[c][:, :1], 0.0)
-        nc.vector.memset(round_bias[:, :1], 0.0)
+        nc.vector.memset(half_bias[:, :1], 0.0)
+        last_bias = keep.tile([P, 1], F32, tag="codes_third", align_bytes=64)
+        nc.vector.memset(last_bias[:], 0.0)
         make_identity(nc, ident[:])
 
         w1_rows = w1.rearrange("(g p j) i -> g p j i", p=P, j=PACK)
         w1_raw = {}
-        raw_place = {
-            (0, 0): (0, 1), (0, 1): (RAW, 1), (1, 0): (2 * RAW, 1), (1, 1): (3 * RAW + RAW // 2, 2),
-            (2, 0): (6 * RAW, 1), (2, 1): (7 * RAW, 1), (3, 0): (8 * RAW, 1), (3, 1): (9 * RAW, 2),
-        }
 
         def load_w1(c, g):
-            start, count = raw_place[(c, g)]
-            raw = early.tile([P, count, PACK, P], F32, name=f"w1_raw{c}_{g}", align_bytes=256, offset=start)
+            offset, units = RAW_PLACE[(c, g)]
+            raw = early.tile([P, units, PACK, P], F32, name=f"w1_raw{c}_{g}", align_bytes=256, offset=offset)
             nc.sync.dma_start(out=raw[:, 0], in_=w1_rows[g][:, :, c * P : (c + 1) * P])
             w1_raw[(c, g)] = raw
 
@@ -145,17 +156,17 @@ def tile_picked_wlapl_gelu_l_kernel(
                     out=h[c][:, halves[s]], in_=pre[s][:], func=GELU, bias=bias[c][:, :1] if c in bias else 0.0
                 )
 
-        def negate(c, offset=None):
-            if offset is None:
-                neg_h[c] = keep.tile([P, T], F32, name=f"neg_h{c}")
+        def negate(c):
+            if c in NEG_PLACE:
+                neg_h[c] = early.tile([P, T], F32, name=f"neg_h{c}", align_bytes=256, offset=NEG_PLACE[c])
             else:
-                neg_h[c] = early.tile([P, T], F32, name=f"neg_h{c}", align_bytes=256, offset=offset)
+                neg_h[c] = keep.tile([P, T], F32, name=f"neg_h{c}")
             nc.scalar.activation(out=neg_h[c][:], in_=h[c][:, :T], func=COPY, scale=-1.0)
 
-        def neighbours(c, v0, width, product_tile, sums=None):
+        def neighbours(c, v0, width, pool, places, sums=None):
             banks = range(v0 // P, (v0 + width) // P)
             sums = sums or {b: zt[b][:, c * P : (c + 1) * P] for b in banks}
-            joins = 1 if c < 2 else 0
+            joins = 1 if c in NEG_PLACE else 0
             for d in range(D):
                 if d == joins:
                     for b in banks:
@@ -163,7 +174,11 @@ def tile_picked_wlapl_gelu_l_kernel(
                             sums[b], neg_h[c][:, b * P : (b + 1) * P], ident[:],
                             start=(d == 0), stop=False, is_transpose=True,
                         )
-                prod = product_tile(d, [P, width], f"prod{c}_{v0}_{d}")
+                name = f"prod{c}_{v0}_{d}"
+                if d in places:
+                    prod = pool.tile([P, width], F32, name=name, align_bytes=64, offset=places[d])
+                else:
+                    prod = keep.tile([P, width], F32, name=name, align_bytes=64)
                 nc.vector.tensor_tensor(
                     prod[:],
                     h[c][:].indirect(lists[d][:, v0 // 16 : (v0 + width) // 16]),
@@ -176,12 +191,8 @@ def tile_picked_wlapl_gelu_l_kernel(
                         start=(d < joins), stop=(d == D - 1), is_transpose=True,
                     )
 
-        def placed(pool, offsets):
-            return lambda d, shape, name: (
-                pool.tile(shape, F32, name=name, align_bytes=256 if pool is early else 64, offset=offsets[d])
-                if d in offsets
-                else keep.tile(shape, F32, name=name, align_bytes=64)
-            )
+        def late_places(first):
+            return {d: (first + d) * SMALL for d in range(D)}
 
         def round_z(c0, count, v0, width, sums=None, zero=None):
             rows = slice(c0 * P // PACK, (c0 + count) * P // PACK)
@@ -208,84 +219,85 @@ def tile_picked_wlapl_gelu_l_kernel(
                     in_=turned[:, b].rearrange("p u v -> p v u"),
                 )
 
-        def finish(v0, z_bf, z_codes, copy_out, bank=None):
-            width = len(z_bf) * P
-            z_scales = keep.tile([P, width], U8, name=f"z_scales{v0}", align_bytes=64)
-            for b in range(len(z_bf)):
-                cols = slice(b * P, (b + 1) * P)
-                nc.vector.quantize_mx(out=z_codes[:, cols].bitcast(FP8X4), scales=z_scales[:, cols], in_=z_bf[b])
-            for m in range(N // P):
-                if bank is None:
-                    acc = psum.tile([P, width], F32, name=f"out_acc{v0}_{m}", tag="acc", bufs=2)[:]
-                else:
-                    acc = bank[:, m * width : (m + 1) * width]
-                nc.tensor.matmul_mx(
-                    out=acc,
-                    lhsT=w2_codes[:, 2 * P * m : 2 * P * (m + 1)].bitcast(FP4X4),
-                    lhsT_scale=w2_plane[:, P * m : P * (m + 1)],
-                    rhs=z_codes[:].bitcast(FP8X4),
-                    rhs_scale=z_scales[:],
-                    start=True,
-                    stop=True,
-                )
-                if bank is None:
-                    result = keep.tile([P, width], F32, name=f"result{v0}_{m}", align_bytes=256)
-                    copy_out[m](out=result[:], in_=acc)
-                    nc.sync.dma_start(out=out[m * P : (m + 1) * P, v0 : v0 + width], in_=result[:])
-            if bank is not None:
-                result = keep.tile([P, N // P, width], F32, name=f"result{v0}", align_bytes=256)
-                copy_out[0](out=result[:].rearrange("p m v -> p (m v)"), in_=bank)
-                nc.sync.dma_start(
-                    out=out.rearrange("(m p) v -> p m v", p=P)[:, :, v0 : v0 + width], in_=result[:]
-                )
+        def quantise_z(v0, z_bf, z_codes):
+            z_scales = keep.tile([P, z_codes.shape[1]], U8, name=f"z_scales{v0}", align_bytes=64)
+            nc.vector.quantize_mx(out=z_codes.bitcast(FP8X4), scales=z_scales[:], in_=z_bf)
+            return z_codes, z_scales[:]
+
+        def multiply(z_mx, m, acc):
+            nc.tensor.matmul_mx(
+                out=acc,
+                lhsT=w2_codes[:, 2 * P * m : 2 * P * (m + 1)].bitcast(FP4X4),
+                lhsT_scale=w2_plane[:, P * m : P * (m + 1)],
+                rhs=z_mx[0].bitcast(FP8X4),
+                rhs_scale=z_mx[1],
+                start=True,
+                stop=True,
+            )
+
+        out_rows = out.rearrange("(m p) v -> p m v", p=P)
+
+        def store(v0, width, m0, count, acc, copy_out):
+            result = keep.tile([P, count, width], F32, name=f"result{v0}_{m0}", align_bytes=256)
+            copy_out(out=result[:].rearrange("p m v -> p (m v)"), in_=acc)
+            nc.sync.dma_start(out=out_rows[:, m0 : m0 + count, v0 : v0 + width], in_=result[:])
 
         on_scalar, on_vector = nc.scalar.copy, nc.vector.tensor_copy
 
         project(0)
         project(1)
-        negate(0, 4 * RAW)
-        neighbours(0, 0, T, placed(early, {2: 3 * RAW, 3: 5 * RAW}))
+        negate(0)
+        neighbours(0, 0, T, early, PRODUCT_PLACE[0])
         project(2)
         project(3)
-        negate(1, 10 * RAW)
-        negate(2)
-        negate(3)
-        neighbours(1, 0, T, placed(early, {2: 7 * RAW, 3: 9 * RAW}))
+        for c in range(1, BLOCKS):
+            negate(c)
+        neighbours(1, 0, T, early, PRODUCT_PLACE[1])
         round_z(0, 2, 0, T)
 
         half_sums = [psum.tile([P, 2 * P], F32, name=f"half_sums{b}", tag=f"spare{b}") for b in range(2)]
         for c in (2, 3):
             sums = {b: half_sums[b][:, (c - 2) * P : (c - 1) * P] for b in range(2)}
-            neighbours(c, 0, HALF, placed(late, {}), sums)
-        round_z(2, 2, 0, HALF, {b: half_sums[b][:] for b in range(2)}, zero=round_bias[:, :1])
-        held = lambda first: placed(late, {d: (first + d) * 4 * QUARTER for d in range(D)})
-        z_held = late.tile(
-            [P, (4 * D - AFTER_QUANTISE) * 2 * QUARTER], BF16, align_bytes=64,
-            offset=AFTER_QUANTISE * 4 * QUARTER,
-        )
-        z_second = keep.tile([P, QUARTER * PACK], BF16, align_bytes=64)
-        z_half = [z_held[:, : QUARTER * PACK], z_second[:]]
-        turn_back(0, z_half, "zt0")
-        codes_half = keep.tile([P, HALF], U32, align_bytes=64)
-        finish(0, z_half, codes_half, (on_scalar, on_scalar))
+            neighbours(c, 0, HALF, late, {}, sums)
+        round_z(2, 2, 0, HALF, {b: half_sums[b][:] for b in range(2)}, zero=half_bias[:, :1])
+        z_half = keep.tile([P, HALF * PACK], BF16, align_bytes=64)
+        turn_back(0, [z_half[:, : QUARTER * PACK], z_half[:, QUARTER * PACK :]], "zt0")
 
         third, fourth = HALF, HALF + QUARTER
-        neighbours(2, third, QUARTER, held(0))
-        neighbours(3, third, QUARTER, held(D))
+        neighbours(2, third, QUARTER, late, late_places(0))
+        neighbours(3, third, QUARTER, late, late_places(D))
         round_z(2, 2, third, QUARTER)
         z_third = keep.tile([P, QUARTER * PACK], BF16, align_bytes=64)
         turn_back(third, [z_third[:]], "spare0")
 
-        neighbours(2, fourth, QUARTER, held(2 * D))
+        neighbours(2, fourth, QUARTER, late, late_places(2 * D))
         round_z(2, 1, fourth, QUARTER)
         last_sums = psum.tile([P, P], F32, tag="zt1")
         sums = {fourth // P: last_sums[:]}
-        neighbours(3, fourth, QUARTER, held(3 * D), sums)
-        round_z(3, 1, fourth, QUARTER, sums)
+        neighbours(3, fourth, QUARTER, late, late_places(3 * D), sums)
+
+        codes_half = keep.tile([P, HALF], U32, tag=f"gate{D - 2}", align_bytes=256)
+        mx_half = quantise_z(0, z_half[:], codes_half[:])
+        acc_half0 = psum.tile([P, HALF], F32, tag="acc", bufs=2)
+        multiply(mx_half, 0, acc_half0[:])
+        store(0, HALF, 0, 1, acc_half0[:], on_vector)
+        round_z(3, 1, fourth, QUARTER, sums, zero=last_bias[:])
         z_fourth = keep.tile([P, QUARTER * PACK], BF16, align_bytes=64)
         turn_back(fourth, [z_fourth[:]], "spare1")
-        codes_third = keep.tile([P, QUARTER], U32, tag=f"gate{D - 2}", align_bytes=256)
-        out_third = psum.tile([P, N // P * QUARTER], F32, tag="zt1")
-        finish(third, [z_third[:]], codes_third, (on_scalar,), out_third[:])
+        acc_half1 = psum.tile([P, HALF], F32, tag="zt1")
+        multiply(mx_half, 1, acc_half1[:])
+        store(0, HALF, 1, 1, acc_half1[:], on_scalar)
+
+        codes_third = keep.tile([P, QUARTER], U32, tag="codes_third", align_bytes=64)
+        mx_third = quantise_z(third, z_third[:], codes_third[:])
+        acc_third = psum.tile([P, N // P * QUARTER], F32, tag="zt2")
+        for m in range(N // P):
+            multiply(mx_third, m, acc_third[:, m * QUARTER : (m + 1) * QUARTER])
+        store(third, QUARTER, 0, N // P, acc_third[:], on_scalar)
+
         codes_fourth = keep.tile([P, QUARTER], U32, align_bytes=64)
-        finish(fourth, [z_fourth[:]], codes_fourth, (on_scalar, on_vector))
+        mx_fourth = quantise_z(fourth, z_fourth[:], codes_fourth[:])
+        for m, copy_out in enumerate((on_vector, on_scalar)):
+            acc = psum.tile([P, QUARTER], F32, name=f"acc_fourth{m}", tag="acc", bufs=2)
+            multiply(mx_fourth, m, acc[:])
+            store(fourth, QUARTER, m, 1, acc[:], copy_out)

@@ -27,6 +27,7 @@ BLOCKS = H // P
 HALF, QUARTER = T // 2, T // 4
 SPARE = 8
 AFTER_ROUND = 7
+WARM_PASSES = 5
 UNIT = 4 * T
 SMALL = 4 * QUARTER
 
@@ -35,13 +36,11 @@ RAW_PLACE = {
     (0, 1): (UNIT, 1),
     (1, 0): (2 * UNIT, 1),
     (1, 1): (3 * UNIT + UNIT // 2, 2),
-    (2, 0): (6 * UNIT, 1),
-    (2, 1): (7 * UNIT, 1),
-    (3, 0): (8 * UNIT, 1),
-    (3, 1): (9 * UNIT, 2),
+    (2, 0): (6 * UNIT, 2),
+    (2, 1): (8 * UNIT, 2),
 }
-PRODUCT_PLACE = {0: {2: 3 * UNIT, 3: 5 * UNIT}, 1: {2: 7 * UNIT, 3: 9 * UNIT}}
-NEG_PLACE = {0: 4 * UNIT, 1: 10 * UNIT}
+PRODUCT_PLACE = {0: {2: 3 * UNIT, 3: 5 * UNIT}, 1: {2: 10 * UNIT, 3: 8 * UNIT}}
+NEG_PLACE = {0: 4 * UNIT, 1: 9 * UNIT}
 
 
 def tile_picked_wlapl_gelu_l_kernel(
@@ -70,11 +69,30 @@ def tile_picked_wlapl_gelu_l_kernel(
         half_bias = late.tile([P, (4 * D - AFTER_ROUND) * QUARTER], F32, align_bytes=64, offset=AFTER_ROUND * SMALL)
         bias[3] = late.tile([P, AFTER_ROUND * QUARTER], F32, name="bias3", align_bytes=64, offset=0)
 
+        warm_in = keep.tile([P, HALF * PACK], BF16, align_bytes=64)
+        warm_codes = keep.tile([P, HALF], U32, align_bytes=64)
+        warm_scales = keep.tile([P, HALF], U8, align_bytes=64)
+        nc.vector.memset(warm_in[:].bitcast(F32), 1.0)
+        nc.vector.quantize_mx(out=warm_codes[:].bitcast(FP8X4), scales=warm_scales[:], in_=warm_in[:])
+        warm_out = psum.tile([P, HALF], F32, tag="spare0")
+        for n in range(WARM_PASSES):
+            nc.tensor.matmul_mx(
+                out=warm_out[:],
+                lhsT=warm_codes[:, :P].bitcast(FP8X4),
+                lhsT_scale=warm_scales[:, :P],
+                rhs=warm_codes[:].bitcast(FP8X4),
+                rhs_scale=warm_scales[:],
+                start=(n == 0),
+                stop=(n == WARM_PASSES - 1),
+            )
+
         nc.gpsimd.memset(x_planes[:].bitcast(I32), 0)
         nc.vector.memset(w2_plane[:].bitcast(I32), 0)
         for c in bias:
             nc.vector.memset(bias[c][:, :1], 0.0)
         nc.vector.memset(half_bias[:, :1], 0.0)
+        cast_bias = early.tile([P, T], F32, align_bytes=256, offset=PRODUCT_PLACE[1][2])
+        nc.vector.memset(cast_bias[:, :1], 0.0)
         last_bias = keep.tile([P, 1], F32, tag="codes_third", align_bytes=64)
         nc.vector.memset(last_bias[:], 0.0)
         make_identity(nc, ident[:])
@@ -84,8 +102,12 @@ def tile_picked_wlapl_gelu_l_kernel(
 
         def load_w1(c, g):
             offset, units = RAW_PLACE[(c, g)]
-            raw = early.tile([P, units, PACK, P], F32, name=f"w1_raw{c}_{g}", align_bytes=256, offset=offset)
-            nc.sync.dma_start(out=raw[:, 0], in_=w1_rows[g][:, :, c * P : (c + 1) * P])
+            if c < 2:
+                raw = early.tile([P, units, PACK, P], F32, name=f"w1_raw{c}_{g}", align_bytes=256, offset=offset)
+                nc.sync.dma_start(out=raw[:, 0], in_=w1_rows[g][:, :, c * P : (c + 1) * P])
+            else:
+                raw = early.tile([P, PACK, 2 * P], F32, name=f"w1_raw{c}_{g}", align_bytes=256, offset=offset)
+                nc.sync.dma_start(out=raw[:], in_=w1_rows[g][:, :, 2 * P :])
             w1_raw[(c, g)] = raw
 
         def load_neighbours(d):
@@ -108,9 +130,8 @@ def tile_picked_wlapl_gelu_l_kernel(
         load_w1(1, 1)
         for d in range(2, D):
             load_neighbours(d)
-        for c in (2, 3):
-            for g in range(PASSES):
-                load_w1(c, g)
+        for g in range(PASSES):
+            load_w1(2, g)
         nc.sync.dma_start(out=w2_codes[:].bitcast(I32), in_=w2_words[0].bitcast(I32))
         w2_scale_rows = w2_scales[0].bitcast(I32).rearrange("(q r) w -> r q w", r=4)
         for r in range(4):
@@ -119,24 +140,39 @@ def tile_picked_wlapl_gelu_l_kernel(
         for c in range(2):
             nc.scalar.activation(out=h[c][:, T:], in_=ident[:, :SPARE], func=GELU)
 
+        upper = []
+
         def project(c):
             width = P * PACK
-            grouped = keep.tile([P, PASSES * width], BF16, name=f"w1_bf{c}", tag=f"w1_bf{c}", align_bytes=64)
+            if c < 2:
+                grouped = keep.tile([P, PASSES * width], BF16, name=f"w1_bf{c}", tag=f"w1_bf{c}", align_bytes=64)[:]
+            else:
+                if c == 2:
+                    upper.append(keep.tile([P, 2 * PASSES * width], BF16, name="w1_bf2", tag="w1_bf2", align_bytes=64))
+                grouped = upper[0][:, (c - 2) * PASSES * width : (c - 1) * PASSES * width]
             codes = keep.tile([P, PASSES * P], U32, name=f"w1_codes{c}", align_bytes=64)
             scales = keep.tile([P, PASSES * P], U8, name=f"w1_scales{c}", align_bytes=64)
             first = c == 0
             cast = nc.vector.tensor_copy if first else nc.scalar.copy
             for g in range(PASSES):
                 part = grouped[:, g * width : (g + 1) * width]
-                cast(
-                    out=part.rearrange("p (a n t) -> p a t n", n=4, t=PACK),
-                    in_=w1_raw[(c, g)][:, 0].rearrange("p t (a n) -> p a t n", n=4),
-                )
+                if c < 2:
+                    cast(
+                        out=part.rearrange("p (a n t) -> p a t n", n=4, t=PACK),
+                        in_=w1_raw[(c, g)][:, 0].rearrange("p t (a n) -> p a t n", n=4),
+                    )
+                else:
+                    nc.scalar.activation(
+                        out=part.rearrange("p (a e t) -> p a t e", e=2, t=PACK),
+                        in_=w1_raw[(2, g)][:].rearrange("p t (a u e) -> p u a t e", u=2, e=2)[:, c - 2],
+                        func=IDENTITY if (c, g) == (2, 1) else COPY,
+                        bias=cast_bias[:, :1] if (c, g) == (2, 1) else 0.0,
+                    )
                 if first:
                     cols = slice(g * P, (g + 1) * P)
                     nc.vector.quantize_mx(out=codes[:, cols].bitcast(FP8X4), scales=scales[:, cols], in_=part)
             if not first:
-                nc.vector.quantize_mx(out=codes[:].bitcast(FP8X4), scales=scales[:], in_=grouped[:])
+                nc.vector.quantize_mx(out=codes[:].bitcast(FP8X4), scales=scales[:], in_=grouped)
             halves = [slice(s * HALF, (s + 1) * HALF) for s in range(2)]
             pre = [psum.tile([P, HALF], F32, name=f"pre{c}_{s}", tag="acc", bufs=2) for s in range(2)]
             for g in range(PASSES):
@@ -197,11 +233,16 @@ def tile_picked_wlapl_gelu_l_kernel(
         def round_z(c0, count, v0, width, sums=None, zero=None):
             rows = slice(c0 * P // PACK, (c0 + count) * P // PACK)
             for b in range(v0 // P, (v0 + width) // P):
+                summed = sums[b] if sums else zt[b][:, c0 * P : (c0 + count) * P]
+                if c0 < 2:
+                    target = zt_bf[b][:].rearrange("v (u p e) -> v u p e", u=2, e=2)[:, :, rows, :]
+                    summed = summed.rearrange("v (p u e) -> v u p e", u=2, e=2)
+                else:
+                    target = zt_bf[b][:].rearrange("v (u s j) -> v u s j", u=2, s=2)[:, c0 - 2 : c0 - 2 + count, 1, :]
+                    summed = summed.rearrange("v (u j) -> v u j", u=count)
                 nc.scalar.activation(
-                    out=zt_bf[b][:].rearrange("v (u p e) -> v u p e", u=2, e=2)[:, :, rows, :],
-                    in_=(sums[b] if sums else zt[b][:, c0 * P : (c0 + count) * P]).rearrange(
-                        "v (p u e) -> v u p e", u=2, e=2
-                    ),
+                    out=target,
+                    in_=summed,
                     func=IDENTITY if zero is not None else COPY,
                     bias=zero if zero is not None else 0.0,
                     scale=-1.0,

@@ -26,7 +26,7 @@ PASSES = K // (P * PACK)
 BLOCKS = H // P
 HALF, QUARTER = T // 2, T // 4
 SPARE = 8
-AFTER_ROUND = 7
+AFTER_ROUND = 8
 WARM_PASSES = 5
 UNIT = 4 * T
 SMALL = 4 * QUARTER
@@ -55,7 +55,7 @@ def tile_picked_wlapl_gelu_l_kernel(
 
         lists = [keep.tile([P, T // 16], U16, name=f"list{d}") for d in range(D)]
         gates = [keep.tile([P, T], F32, name=f"gate{d}", tag=f"gate{d}", align_bytes=256) for d in range(D)]
-        x_codes = [keep.tile([P, T], U32, name=f"x_codes{g}", align_bytes=256) for g in range(PASSES)]
+        x_codes = [keep.tile([P, PASSES * HALF], U32, name=f"x_codes{s}", align_bytes=256) for s in range(2)]
         x_planes = keep.tile([P, PASSES * T], U8, align_bytes=256)
         w2_codes = keep.tile([P, 2 * N], U8, align_bytes=64)
         w2_plane = keep.tile([P, N], U8, align_bytes=64)
@@ -120,9 +120,11 @@ def tile_picked_wlapl_gelu_l_kernel(
         x_scale_rows = x_scales.bitcast(I32).rearrange("g (q r) w -> r q g w", r=4)
         for r in range(4):
             nc.sync.dma_start(out=x_plane_words[r:P:32], in_=x_scale_rows[r])
-        for g in range(PASSES):
+        x_rows = x_words.rearrange("g p n t -> p g (n t)").bitcast(I32)
+        for s in range(2):
             nc.sync.dma_start(
-                out=x_codes[g][:].bitcast(I32), in_=x_words[g].rearrange("p n t -> p (n t)").bitcast(I32)
+                out=x_codes[s][:].bitcast(I32).rearrange("p (g n) -> p g n", g=PASSES),
+                in_=x_rows[:, :, s * HALF : (s + 1) * HALF],
             )
         load_neighbours(0)
         load_w1(1, 0)
@@ -138,7 +140,7 @@ def tile_picked_wlapl_gelu_l_kernel(
             nc.sync.dma_start(out=w2_plane[:].bitcast(I32)[r:P:32], in_=w2_scale_rows[r])
 
         for c in range(2):
-            nc.scalar.activation(out=h[c][:, T:], in_=ident[:, :SPARE], func=GELU)
+            nc.scalar.activation(out=h[c][:, T:], in_=warm_in[:].bitcast(F32)[:, :SPARE], func=GELU)
 
         upper = []
 
@@ -157,10 +159,13 @@ def tile_picked_wlapl_gelu_l_kernel(
             for g in range(PASSES):
                 part = grouped[:, g * width : (g + 1) * width]
                 if c < 2:
-                    cast(
-                        out=part.rearrange("p (a n t) -> p a t n", n=4, t=PACK),
-                        in_=w1_raw[(c, g)][:, 0].rearrange("p t (a n) -> p a t n", n=4),
-                    )
+                    target = part.rearrange("p (a n t) -> p a t n", n=4, t=PACK)
+                    source = w1_raw[(c, g)][:, 0].rearrange("p t (a n) -> p a t n", n=4)
+                    if (c, g) == (0, 1):
+                        nc.vector.tensor_copy(out=target[:, :16], in_=source[:, :16])
+                        nc.scalar.copy(out=target[:, 16:], in_=source[:, 16:])
+                    else:
+                        cast(out=target, in_=source)
                 else:
                     nc.scalar.activation(
                         out=part.rearrange("p (a e t) -> p a t e", e=2, t=PACK),
@@ -175,14 +180,15 @@ def tile_picked_wlapl_gelu_l_kernel(
                 nc.vector.quantize_mx(out=codes[:].bitcast(FP8X4), scales=scales[:], in_=grouped)
             halves = [slice(s * HALF, (s + 1) * HALF) for s in range(2)]
             pre = [psum.tile([P, HALF], F32, name=f"pre{c}_{s}", tag="acc", bufs=2) for s in range(2)]
-            for g in range(PASSES):
+            steps = [(g, s) for g in range(PASSES) for s in range(2)]
+            for g, s in sorted(steps, key=lambda step: step[1]) if first else steps:
                 cols = slice(g * P, (g + 1) * P)
-                for s in range(2):
+                if True:
                     nc.tensor.matmul_mx(
                         out=pre[s][:],
                         lhsT=codes[:, cols].bitcast(FP8X4),
                         lhsT_scale=scales[:, cols],
-                        rhs=x_codes[g][:, halves[s]].bitcast(FP8X4),
+                        rhs=x_codes[s][:, halves[g]].bitcast(FP8X4),
                         rhs_scale=x_planes[:, g * T : (g + 1) * T][:, halves[s]],
                         start=(g == 0),
                         stop=(g == PASSES - 1),
@@ -305,14 +311,15 @@ def tile_picked_wlapl_gelu_l_kernel(
         turn_back(0, [z_half[:, : QUARTER * PACK], z_half[:, QUARTER * PACK :]], "zt0")
 
         third, fourth = HALF, HALF + QUARTER
-        neighbours(2, third, QUARTER, late, late_places(0))
-        neighbours(3, third, QUARTER, late, late_places(D))
-        round_z(2, 2, third, QUARTER)
+        neighbours(2, third, HALF, late, {d: 2 * d * SMALL for d in range(D)})
+        round_z(2, 1, third, HALF)
+        third_sums = psum.tile([P, P], F32, tag="acc", bufs=2)
+        sums = {third // P: third_sums[:]}
+        neighbours(3, third, QUARTER, late, late_places(2 * D), sums)
+        round_z(3, 1, third, QUARTER, sums)
         z_third = keep.tile([P, QUARTER * PACK], BF16, align_bytes=64)
         turn_back(third, [z_third[:]], "spare0")
 
-        neighbours(2, fourth, QUARTER, late, late_places(2 * D))
-        round_z(2, 1, fourth, QUARTER)
         last_sums = psum.tile([P, P], F32, tag="zt1")
         sums = {fourth // P: last_sums[:]}
         neighbours(3, fourth, QUARTER, late, late_places(3 * D), sums)

@@ -26,7 +26,7 @@ PASSES = K // (P * PACK)
 BLOCKS = H // P
 HALF, QUARTER = T // 2, T // 4
 SPARE = 8
-AFTER_ROUND = 8
+AFTER_ROUND = 6
 WARM_PASSES = 5
 UNIT = 4 * T
 SMALL = 4 * QUARTER
@@ -66,7 +66,7 @@ def tile_picked_wlapl_gelu_l_kernel(
         zt_bf = [keep.tile([P, H], BF16, name=f"zt_bf{b}") for b in range(T // P)]
 
         bias = {c: keep.tile([P, 1], F32, name=f"bias{c}", tag=f"w1_bf{c + 1}", align_bytes=64) for c in range(2)}
-        half_bias = late.tile([P, (4 * D - AFTER_ROUND) * QUARTER], F32, align_bytes=64, offset=AFTER_ROUND * SMALL)
+        half_bias = late.tile([P, (3 * D - AFTER_ROUND) * QUARTER], F32, align_bytes=64, offset=AFTER_ROUND * SMALL)
         bias[3] = late.tile([P, AFTER_ROUND * QUARTER], F32, name="bias3", align_bytes=64, offset=0)
 
         warm_in = keep.tile([P, HALF * PACK], BF16, align_bytes=64)
@@ -142,57 +142,63 @@ def tile_picked_wlapl_gelu_l_kernel(
         for c in range(2):
             nc.scalar.activation(out=h[c][:, T:], in_=warm_in[:].bitcast(F32)[:, :SPARE], func=GELU)
 
-        upper = []
+        width_bf = PASSES * P * PACK
+        w1_bf = {}
+
+        def cast_w1(c, g, part):
+            if c >= 2:
+                held = (c, g) == (2, PASSES - 1)
+                nc.scalar.activation(
+                    out=part.rearrange("p (a e t) -> p a t e", e=2, t=PACK),
+                    in_=w1_raw[(2, g)][:].rearrange("p t (a u e) -> p u a t e", u=2, e=2)[:, c - 2],
+                    func=IDENTITY if held else COPY,
+                    bias=cast_bias[:, :1] if held else 0.0,
+                )
+                return
+            target = part.rearrange("p (a n t) -> p a t n", n=4, t=PACK)
+            source = w1_raw[(c, g)][:, 0].rearrange("p t (a n) -> p a t n", n=4)
+            if c == 1:
+                nc.scalar.copy(out=target, in_=source)
+            elif g < PASSES - 1:
+                nc.vector.tensor_copy(out=target, in_=source)
+            else:
+                share = P // 4 // 2
+                nc.vector.tensor_copy(out=target[:, :share], in_=source[:, :share])
+                nc.scalar.copy(out=target[:, share:], in_=source[:, share:])
 
         def project(c):
-            width = P * PACK
-            if c < 2:
-                grouped = keep.tile([P, PASSES * width], BF16, name=f"w1_bf{c}", tag=f"w1_bf{c}", align_bytes=64)[:]
-            else:
-                if c == 2:
-                    upper.append(keep.tile([P, 2 * PASSES * width], BF16, name="w1_bf2", tag="w1_bf2", align_bytes=64))
-                grouped = upper[0][:, (c - 2) * PASSES * width : (c - 1) * PASSES * width]
+            if c < 3:
+                count = 1 if c < 2 else 2
+                tile = keep.tile([P, count * width_bf], BF16, name=f"w1_bf{c}", tag=f"w1_bf{c}", align_bytes=64)
+                for n in range(count):
+                    w1_bf[c + n] = tile[:, n * width_bf : (n + 1) * width_bf]
             codes = keep.tile([P, PASSES * P], U32, name=f"w1_codes{c}", align_bytes=64)
             scales = keep.tile([P, PASSES * P], U8, name=f"w1_scales{c}", align_bytes=64)
-            first = c == 0
-            cast = nc.vector.tensor_copy if first else nc.scalar.copy
             for g in range(PASSES):
-                part = grouped[:, g * width : (g + 1) * width]
-                if c < 2:
-                    target = part.rearrange("p (a n t) -> p a t n", n=4, t=PACK)
-                    source = w1_raw[(c, g)][:, 0].rearrange("p t (a n) -> p a t n", n=4)
-                    if (c, g) == (0, 1):
-                        nc.vector.tensor_copy(out=target[:, :16], in_=source[:, :16])
-                        nc.scalar.copy(out=target[:, 16:], in_=source[:, 16:])
-                    else:
-                        cast(out=target, in_=source)
-                else:
-                    nc.scalar.activation(
-                        out=part.rearrange("p (a e t) -> p a t e", e=2, t=PACK),
-                        in_=w1_raw[(2, g)][:].rearrange("p t (a u e) -> p u a t e", u=2, e=2)[:, c - 2],
-                        func=IDENTITY if (c, g) == (2, 1) else COPY,
-                        bias=cast_bias[:, :1] if (c, g) == (2, 1) else 0.0,
-                    )
-                if first:
+                part = w1_bf[c][:, g * P * PACK : (g + 1) * P * PACK]
+                cast_w1(c, g, part)
+                if c == 0:
                     cols = slice(g * P, (g + 1) * P)
                     nc.vector.quantize_mx(out=codes[:, cols].bitcast(FP8X4), scales=scales[:, cols], in_=part)
-            if not first:
-                nc.vector.quantize_mx(out=codes[:].bitcast(FP8X4), scales=scales[:], in_=grouped)
+            if c > 0:
+                nc.vector.quantize_mx(out=codes[:].bitcast(FP8X4), scales=scales[:], in_=w1_bf[c])
             halves = [slice(s * HALF, (s + 1) * HALF) for s in range(2)]
             pre = [psum.tile([P, HALF], F32, name=f"pre{c}_{s}", tag="acc", bufs=2) for s in range(2)]
-            steps = [(g, s) for g in range(PASSES) for s in range(2)]
-            for g, s in sorted(steps, key=lambda step: step[1]) if first else steps:
+            if c == 0:
+                steps = [(g, s) for s in range(2) for g in range(PASSES)]
+            else:
+                steps = [(g, s) for g in range(PASSES) for s in range(2)]
+            for g, s in steps:
                 cols = slice(g * P, (g + 1) * P)
-                if True:
-                    nc.tensor.matmul_mx(
-                        out=pre[s][:],
-                        lhsT=codes[:, cols].bitcast(FP8X4),
-                        lhsT_scale=scales[:, cols],
-                        rhs=x_codes[s][:, halves[g]].bitcast(FP8X4),
-                        rhs_scale=x_planes[:, g * T : (g + 1) * T][:, halves[s]],
-                        start=(g == 0),
-                        stop=(g == PASSES - 1),
-                    )
+                nc.tensor.matmul_mx(
+                    out=pre[s][:],
+                    lhsT=codes[:, cols].bitcast(FP8X4),
+                    lhsT_scale=scales[:, cols],
+                    rhs=x_codes[s][:, g * HALF : (g + 1) * HALF].bitcast(FP8X4),
+                    rhs_scale=x_planes[:, g * T : (g + 1) * T][:, halves[s]],
+                    start=(g == 0),
+                    stop=(g == PASSES - 1),
+                )
             for s in range(2):
                 nc.scalar.activation(
                     out=h[c][:, halves[s]], in_=pre[s][:], func=GELU, bias=bias[c][:, :1] if c in bias else 0.0
@@ -205,16 +211,21 @@ def tile_picked_wlapl_gelu_l_kernel(
                 neg_h[c] = keep.tile([P, T], F32, name=f"neg_h{c}")
             nc.scalar.activation(out=neg_h[c][:], in_=h[c][:, :T], func=COPY, scale=-1.0)
 
-        def neighbours(c, v0, width, pool, places, sums=None):
+        def neighbours(c, v0, width, pool, places, bank=None):
             banks = range(v0 // P, (v0 + width) // P)
-            sums = sums or {b: zt[b][:, c * P : (c + 1) * P] for b in banks}
+            if bank is None:
+                sums = {b: zt[b][:, c * P : (c + 1) * P] for b in banks}
+                opens = closes = banks
+            else:
+                sums = {b: bank[:, b * P - v0 : (b + 1) * P - v0] for b in banks}
+                opens, closes = banks[:1], banks[-1:]
             joins = 1 if c in NEG_PLACE else 0
             for d in range(D):
                 if d == joins:
                     for b in banks:
                         nc.tensor.matmul(
                             sums[b], neg_h[c][:, b * P : (b + 1) * P], ident[:],
-                            start=(d == 0), stop=False, is_transpose=True,
+                            start=(d == 0 and b in opens), stop=False, is_transpose=True,
                         )
                 name = f"prod{c}_{v0}_{d}"
                 if d in places:
@@ -230,17 +241,20 @@ def tile_picked_wlapl_gelu_l_kernel(
                 for b in banks:
                     nc.tensor.matmul(
                         sums[b], prod[:, b * P - v0 : (b + 1) * P - v0], ident[:],
-                        start=(d < joins), stop=(d == D - 1), is_transpose=True,
+                        start=(d < joins and b in opens), stop=(d == D - 1 and b in closes), is_transpose=True,
                     )
 
         def late_places(first):
             return {d: (first + d) * SMALL for d in range(D)}
 
-        def round_z(c0, count, v0, width, sums=None, zero=None):
-            rows = slice(c0 * P // PACK, (c0 + count) * P // PACK)
+        def round_z(c0, count, v0, width, bank=None, zero=None):
             for b in range(v0 // P, (v0 + width) // P):
-                summed = sums[b] if sums else zt[b][:, c0 * P : (c0 + count) * P]
+                if bank is None:
+                    summed = zt[b][:, c0 * P : (c0 + count) * P]
+                else:
+                    summed = bank[:, b * P - v0 : (b + 1) * P - v0]
                 if c0 < 2:
+                    rows = slice(c0 * P // PACK, (c0 + count) * P // PACK)
                     target = zt_bf[b][:].rearrange("v (u p e) -> v u p e", u=2, e=2)[:, :, rows, :]
                     summed = summed.rearrange("v (p u e) -> v u p e", u=2, e=2)
                 else:
@@ -302,34 +316,33 @@ def tile_picked_wlapl_gelu_l_kernel(
         neighbours(1, 0, T, early, PRODUCT_PLACE[1])
         round_z(0, 2, 0, T)
 
-        half_sums = [psum.tile([P, 2 * P], F32, name=f"half_sums{b}", tag=f"spare{b}") for b in range(2)]
-        for c in (2, 3):
-            sums = {b: half_sums[b][:, (c - 2) * P : (c - 1) * P] for b in range(2)}
-            neighbours(c, 0, HALF, late, {}, sums)
-        round_z(2, 2, 0, HALF, {b: half_sums[b][:] for b in range(2)}, zero=half_bias[:, :1])
+        third, fourth = HALF, HALF + QUARTER
+        lower_sums = psum.tile([P, fourth], F32, tag="spare0")
+        neighbours(2, 0, fourth, late, {}, lower_sums[:])
+        round_z(2, 1, 0, fourth, lower_sums[:])
+        half_sums = psum.tile([P, HALF], F32, tag="spare1")
+        neighbours(3, 0, HALF, late, {}, half_sums[:])
+        round_z(3, 1, 0, HALF, half_sums[:], zero=half_bias[:, :1])
         z_half = keep.tile([P, HALF * PACK], BF16, align_bytes=64)
         turn_back(0, [z_half[:, : QUARTER * PACK], z_half[:, QUARTER * PACK :]], "zt0")
 
-        third, fourth = HALF, HALF + QUARTER
-        neighbours(2, third, HALF, late, {d: 2 * d * SMALL for d in range(D)})
-        round_z(2, 1, third, HALF)
         third_sums = psum.tile([P, P], F32, tag="acc", bufs=2)
-        sums = {third // P: third_sums[:]}
-        neighbours(3, third, QUARTER, late, late_places(2 * D), sums)
-        round_z(3, 1, third, QUARTER, sums)
+        neighbours(3, third, QUARTER, late, late_places(0), third_sums[:])
+        round_z(3, 1, third, QUARTER, third_sums[:])
         z_third = keep.tile([P, QUARTER * PACK], BF16, align_bytes=64)
         turn_back(third, [z_third[:]], "spare0")
 
+        neighbours(2, fourth, QUARTER, late, late_places(D))
+        round_z(2, 1, fourth, QUARTER)
         last_sums = psum.tile([P, P], F32, tag="zt1")
-        sums = {fourth // P: last_sums[:]}
-        neighbours(3, fourth, QUARTER, late, late_places(3 * D), sums)
+        neighbours(3, fourth, QUARTER, late, late_places(2 * D), last_sums[:])
 
         codes_half = keep.tile([P, HALF], U32, tag=f"gate{D - 2}", align_bytes=256)
         mx_half = quantise_z(0, z_half[:], codes_half[:])
         acc_half0 = psum.tile([P, HALF], F32, tag="acc", bufs=2)
         multiply(mx_half, 0, acc_half0[:])
         store(0, HALF, 0, 1, acc_half0[:], on_vector)
-        round_z(3, 1, fourth, QUARTER, sums, zero=last_bias[:])
+        round_z(3, 1, fourth, QUARTER, last_sums[:], zero=last_bias[:])
         z_fourth = keep.tile([P, QUARTER * PACK], BF16, align_bytes=64)
         turn_back(fourth, [z_fourth[:]], "spare1")
         acc_half1 = psum.tile([P, HALF], F32, tag="zt1")

@@ -19,6 +19,7 @@ GELU = mybir.ActivationFunctionType.Gelu_apprx_tanh
 COPY = mybir.ActivationFunctionType.Copy
 IDENTITY = mybir.ActivationFunctionType.Identity
 MULT = mybir.AluOpType.mult
+ADD = mybir.AluOpType.add
 
 P = 128
 PACK = 4
@@ -247,7 +248,7 @@ def tile_picked_wlapl_gelu_l_kernel(
         def late_places(first):
             return {d: (first + d) * SMALL for d in range(D)}
 
-        def round_z(c0, count, v0, width, bank=None, zero=None):
+        def round_z(c0, count, v0, width, bank=None, zero=None, on_vector=False):
             for b in range(v0 // P, (v0 + width) // P):
                 if bank is None:
                     summed = zt[b][:, c0 * P : (c0 + count) * P]
@@ -260,6 +261,9 @@ def tile_picked_wlapl_gelu_l_kernel(
                 else:
                     target = zt_bf[b][:].rearrange("v (u s j) -> v u s j", u=2, s=2)[:, c0 - 2 : c0 - 2 + count, 1, :]
                     summed = summed.rearrange("v (u j) -> v u j", u=count)
+                if on_vector:
+                    nc.vector.tensor_scalar(target, summed, -1.0, zero, MULT, ADD)
+                    continue
                 nc.scalar.activation(
                     out=target,
                     in_=summed,
@@ -341,16 +345,16 @@ def tile_picked_wlapl_gelu_l_kernel(
         mx_half = quantise_z(0, z_half[:], codes_half[:])
         acc_half0 = psum.tile([P, HALF], F32, tag="acc", bufs=2)
         multiply(mx_half, 0, acc_half0[:])
+        round_z(3, 1, fourth, QUARTER, last_sums[:], zero=last_bias[:], on_vector=True)
+        codes_third = keep.tile([P, QUARTER], U32, tag="codes_third", align_bytes=64)
+        mx_third = quantise_z(third, z_third[:], codes_third[:])
         store(0, HALF, 0, 1, acc_half0[:], on_vector)
-        round_z(3, 1, fourth, QUARTER, last_sums[:], zero=last_bias[:])
         z_fourth = keep.tile([P, QUARTER * PACK], BF16, align_bytes=64)
         turn_back(fourth, [z_fourth[:]], "spare1")
         acc_half1 = psum.tile([P, HALF], F32, tag="zt1")
         multiply(mx_half, 1, acc_half1[:])
         store(0, HALF, 1, 1, acc_half1[:], on_scalar)
 
-        codes_third = keep.tile([P, QUARTER], U32, tag="codes_third", align_bytes=64)
-        mx_third = quantise_z(third, z_third[:], codes_third[:])
         acc_third = psum.tile([P, N // P * QUARTER], F32, tag="zt2")
         for m in range(N // P):
             multiply(mx_third, m, acc_third[:, m * QUARTER : (m + 1) * QUARTER])

@@ -272,21 +272,30 @@ def tile_picked_wlapl_gelu_l_kernel(
                     scale=-1.0,
                 )
 
-        def turn_back(v0, z_bf, tag):
+        def turn_back(v0, z_bf, tag, parts=1):
             turned = psum.tile([P, len(z_bf), 2, P], F32, name=f"turned{v0}", tag=tag)
             for b in range(len(z_bf)):
                 words = zt_bf[v0 // P + b][:].bitcast(F32)
                 for u in range(2):
                     nc.tensor.transpose(turned[:, b, u, :], words[:, u * P : (u + 1) * P], ident[:])
+            width = P // parts
             for b in range(len(z_bf)):
-                nc.scalar.copy(
-                    out=z_bf[b].bitcast(F32).rearrange("p (v u) -> p v u", u=2),
-                    in_=turned[:, b].rearrange("p u v -> p v u"),
-                )
+                for n in range(parts):
+                    nc.scalar.copy(
+                        out=z_bf[b].bitcast(F32).rearrange("p (v u) -> p v u", u=2)[:, n * width : (n + 1) * width],
+                        in_=turned[:, b].rearrange("p u v -> p v u")[:, n * width : (n + 1) * width],
+                    )
 
-        def quantise_z(v0, z_bf, z_codes):
+        def quantise_z(v0, z_bf, z_codes, parts=1):
             z_scales = keep.tile([P, z_codes.shape[1]], U8, name=f"z_scales{v0}", align_bytes=64)
-            nc.vector.quantize_mx(out=z_codes.bitcast(FP8X4), scales=z_scales[:], in_=z_bf)
+            width = z_codes.shape[1] // parts
+            for n in range(parts):
+                cols = slice(n * width, (n + 1) * width)
+                nc.vector.quantize_mx(
+                    out=z_codes[:, cols].bitcast(FP8X4),
+                    scales=z_scales[:, cols],
+                    in_=z_bf[:, n * width * PACK : (n + 1) * width * PACK],
+                )
             return z_codes, z_scales[:]
 
         def multiply(z_mx, m, acc):
@@ -350,7 +359,7 @@ def tile_picked_wlapl_gelu_l_kernel(
         mx_third = quantise_z(third, z_third[:], codes_third[:])
         store(0, HALF, 0, 1, acc_half0[:], on_vector)
         z_fourth = keep.tile([P, QUARTER * PACK], BF16, align_bytes=64)
-        turn_back(fourth, [z_fourth[:]], "spare1")
+        turn_back(fourth, [z_fourth[:]], "spare1", parts=2)
         acc_half1 = psum.tile([P, HALF], F32, tag="zt1")
         multiply(mx_half, 1, acc_half1[:])
         store(0, HALF, 1, 1, acc_half1[:], on_scalar)
@@ -361,7 +370,7 @@ def tile_picked_wlapl_gelu_l_kernel(
         store(third, QUARTER, 0, N // P, acc_third[:], on_scalar)
 
         codes_fourth = keep.tile([P, QUARTER], U32, align_bytes=64)
-        mx_fourth = quantise_z(fourth, z_fourth[:], codes_fourth[:])
+        mx_fourth = quantise_z(fourth, z_fourth[:], codes_fourth[:], parts=2)
         for m, copy_out in enumerate((on_vector, on_scalar)):
             acc = psum.tile([P, QUARTER], F32, name=f"acc_fourth{m}", tag="acc", bufs=2)
             multiply(mx_fourth, m, acc[:])

@@ -17,9 +17,7 @@ FP8X4 = mybir.dt.float8_e4m3fn_x4
 FP4X4 = mybir.dt.float4_e2m1fn_x4
 GELU = mybir.ActivationFunctionType.Gelu_apprx_tanh
 COPY = mybir.ActivationFunctionType.Copy
-IDENTITY = mybir.ActivationFunctionType.Identity
 MULT = mybir.AluOpType.mult
-ADD = mybir.AluOpType.add
 
 P = 128
 PACK = 4
@@ -27,21 +25,12 @@ PASSES = K // (P * PACK)
 BLOCKS = H // P
 HALF, QUARTER = T // 2, T // 4
 SPARE = 8
-AFTER_ROUND = 6
-WARM_PASSES = 5
+FUSED = 2
 UNIT = 4 * T
-SMALL = 4 * QUARTER
 
-RAW_PLACE = {
-    (0, 0): (0, 1),
-    (0, 1): (UNIT, 1),
-    (1, 0): (2 * UNIT, 1),
-    (1, 1): (3 * UNIT + UNIT // 2, 2),
-    (2, 0): (6 * UNIT, 2),
-    (2, 1): (8 * UNIT, 2),
-}
-PRODUCT_PLACE = {0: {2: 3 * UNIT, 3: 5 * UNIT}, 1: {2: 10 * UNIT, 3: 8 * UNIT}}
-NEG_PLACE = {0: 4 * UNIT, 1: 9 * UNIT}
+RAW_PLACE = {(0, 0): 0, (0, 1): UNIT, (1, 0): 2 * UNIT, (1, 1): 3 * UNIT, (2, 0): 4 * UNIT, (2, 1): 7 * UNIT}
+PRODUCT_PLACE = {(0, 1): 3 * UNIT, (1, 0): 6 * UNIT + UNIT // 2, (1, 1): 8 * UNIT + UNIT // 2}
+FETCH_PLACE = {(1, 2): 7 * UNIT + UNIT // 2, (0, 3): 10 * UNIT, (1, 3): 10 * UNIT}
 
 
 def tile_picked_wlapl_gelu_l_kernel(
@@ -51,69 +40,41 @@ def tile_picked_wlapl_gelu_l_kernel(
     with ExitStack() as ctx:
         keep = ctx.enter_context(tc.tile_pool(name="keep", bufs=1))
         early = ctx.enter_context(tc.tile_pool(name="early", bufs=1))
-        late = ctx.enter_context(tc.tile_pool(name="late", bufs=1))
         psum = ctx.enter_context(tc.psum_pool(name="psum", bufs=1))
 
         lists = [keep.tile([P, T // 16], U16, name=f"list{d}") for d in range(D)]
-        gates = [keep.tile([P, T], F32, name=f"gate{d}", tag=f"gate{d}", align_bytes=256) for d in range(D)]
+        gates = [keep.tile([P, T], F32, name=f"gate{d}", align_bytes=256) for d in range(D)]
+        neg_gates = [keep.tile([P, T], F32, name=f"neg_gate{d}", align_bytes=256) for d in range(FUSED)]
         x_codes = [keep.tile([P, PASSES * HALF], U32, name=f"x_codes{s}", align_bytes=256) for s in range(2)]
         x_planes = keep.tile([P, PASSES * T], U8, align_bytes=256)
         w2_codes = keep.tile([P, 2 * N], U8, align_bytes=64)
         w2_plane = keep.tile([P, N], U8, align_bytes=64)
         ident = keep.tile([P, P], F32)
+        zeros = keep.tile([P, SPARE], F32)
         h = [keep.tile([P, T + SPARE if c < 2 else T], F32, name=f"h{c}") for c in range(BLOCKS)]
-        neg_h = {}
-        zt = [psum.tile([P, H], F32, name=f"zt{b}", tag=f"zt{b}") for b in range(T // P)]
-        zt_bf = [keep.tile([P, H], BF16, name=f"zt_bf{b}") for b in range(T // P)]
-
-        bias = {c: keep.tile([P, 1], F32, name=f"bias{c}", tag=f"w1_bf{c + 1}", align_bytes=64) for c in range(2)}
-        half_bias = late.tile([P, (3 * D - AFTER_ROUND) * QUARTER], F32, align_bytes=64, offset=AFTER_ROUND * SMALL)
-        bias[3] = late.tile([P, AFTER_ROUND * QUARTER], F32, name="bias3", align_bytes=64, offset=0)
-
-        warm_in = keep.tile([P, HALF * PACK], BF16, align_bytes=64)
-        warm_codes = keep.tile([P, HALF], U32, align_bytes=64)
-        warm_scales = keep.tile([P, HALF], U8, align_bytes=64)
-        nc.vector.memset(warm_in[:].bitcast(F32), 1.0)
-        nc.vector.quantize_mx(out=warm_codes[:].bitcast(FP8X4), scales=warm_scales[:], in_=warm_in[:])
-        warm_out = psum.tile([P, HALF], F32, tag="spare0")
-        for n in range(WARM_PASSES):
-            nc.tensor.matmul_mx(
-                out=warm_out[:],
-                lhsT=warm_codes[:, :P].bitcast(FP8X4),
-                lhsT_scale=warm_scales[:, :P],
-                rhs=warm_codes[:].bitcast(FP8X4),
-                rhs_scale=warm_scales[:],
-                start=(n == 0),
-                stop=(n == WARM_PASSES - 1),
-            )
+        zt_bf = keep.tile([P, T // P * H], BF16, align_bytes=64)
 
         nc.gpsimd.memset(x_planes[:].bitcast(I32), 0)
+        nc.vector.memset(zeros[:], 0.0)
         nc.vector.memset(w2_plane[:].bitcast(I32), 0)
-        for c in bias:
-            nc.vector.memset(bias[c][:, :1], 0.0)
-        nc.vector.memset(half_bias[:, :1], 0.0)
-        cast_bias = early.tile([P, T], F32, align_bytes=256, offset=PRODUCT_PLACE[1][2])
-        nc.vector.memset(cast_bias[:, :1], 0.0)
-        last_bias = keep.tile([P, 1], F32, tag="codes_third", align_bytes=64)
-        nc.vector.memset(last_bias[:], 0.0)
         make_identity(nc, ident[:])
 
         w1_rows = w1.rearrange("(g p j) i -> g p j i", p=P, j=PACK)
         w1_raw = {}
 
         def load_w1(c, g):
-            offset, units = RAW_PLACE[(c, g)]
-            if c < 2:
-                raw = early.tile([P, units, PACK, P], F32, name=f"w1_raw{c}_{g}", align_bytes=256, offset=offset)
-                nc.sync.dma_start(out=raw[:, 0], in_=w1_rows[g][:, :, c * P : (c + 1) * P])
-            else:
-                raw = early.tile([P, PACK, 2 * P], F32, name=f"w1_raw{c}_{g}", align_bytes=256, offset=offset)
-                nc.sync.dma_start(out=raw[:], in_=w1_rows[g][:, :, 2 * P :])
+            cols = slice(c * P, (c + 1) * P) if c < 2 else slice(2 * P, H)
+            raw = early.tile(
+                [P, PACK, cols.stop - cols.start], F32, name=f"w1_raw{c}_{g}", align_bytes=256, offset=RAW_PLACE[(c, g)]
+            )
+            nc.sync.dma_start(out=raw[:], in_=w1_rows[g][:, :, cols])
             w1_raw[(c, g)] = raw
 
-        def load_neighbours(d):
-            nc.sync.dma_start(out=gates[d][:], in_=gate[d])
+        def load_list(d):
             nc.sync.dma_start(lists[d][:], (pos1, pos2, pos3, pos4)[d])
+
+        def load_gate(d):
+            nc.sync.dma_start(out=gates[d][:], in_=gate[d])
 
         load_w1(0, 0)
         load_w1(0, 1)
@@ -127,64 +88,63 @@ def tile_picked_wlapl_gelu_l_kernel(
                 out=x_codes[s][:].bitcast(I32).rearrange("p (g n) -> p g n", g=PASSES),
                 in_=x_rows[:, :, s * HALF : (s + 1) * HALF],
             )
-        load_neighbours(0)
         load_w1(1, 0)
-        load_neighbours(1)
+        load_list(2)
+        load_gate(0)
+        load_list(0)
         load_w1(1, 1)
-        for d in range(2, D):
-            load_neighbours(d)
-        for g in range(PASSES):
-            load_w1(2, g)
+        load_list(3)
+        load_gate(1)
+        load_list(1)
+        load_w1(2, 0)
+        load_gate(2)
+        load_w1(2, 1)
+        load_gate(3)
         nc.sync.dma_start(out=w2_codes[:].bitcast(I32), in_=w2_words[0].bitcast(I32))
         w2_scale_rows = w2_scales[0].bitcast(I32).rearrange("(q r) w -> r q w", r=4)
         for r in range(4):
             nc.sync.dma_start(out=w2_plane[:].bitcast(I32)[r:P:32], in_=w2_scale_rows[r])
 
         for c in range(2):
-            nc.scalar.activation(out=h[c][:, T:], in_=warm_in[:].bitcast(F32)[:, :SPARE], func=GELU)
+            nc.scalar.activation(out=h[c][:, T:], in_=zeros[:], func=GELU)
 
-        width_bf = PASSES * P * PACK
-        w1_bf = {}
+        on_scalar, on_vector = nc.scalar.copy, nc.vector.tensor_copy
+        pass_bf = P * PACK
+        w1_bf = [keep.tile([P, PASSES * pass_bf], BF16, name=f"w1_bf{c}", align_bytes=64) for c in range(2)]
+        w1_bf_upper = keep.tile([P, 2 * PASSES * pass_bf], BF16, align_bytes=64)
+        w1_codes = [keep.tile([P, PASSES * P], U32, name=f"w1_codes{c}", align_bytes=64) for c in range(BLOCKS)]
+        w1_scales = [keep.tile([P, PASSES * P], U8, name=f"w1_scales{c}", align_bytes=64) for c in range(BLOCKS)]
 
-        def cast_w1(c, g, part):
-            if c >= 2:
-                held = (c, g) == (2, PASSES - 1)
-                nc.scalar.activation(
-                    out=part.rearrange("p (a e t) -> p a t e", e=2, t=PACK),
-                    in_=w1_raw[(2, g)][:].rearrange("p t (a u e) -> p u a t e", u=2, e=2)[:, c - 2],
-                    func=IDENTITY if held else COPY,
-                    bias=cast_bias[:, :1] if held else 0.0,
-                )
-                return
-            target = part.rearrange("p (a n t) -> p a t n", n=4, t=PACK)
-            source = w1_raw[(c, g)][:, 0].rearrange("p t (a n) -> p a t n", n=4)
-            if c == 1:
-                nc.scalar.copy(out=target, in_=source)
-            elif g < PASSES - 1:
-                nc.vector.tensor_copy(out=target, in_=source)
-            else:
-                share = P // 4 // 2
-                nc.vector.tensor_copy(out=target[:, :share], in_=source[:, :share])
-                nc.scalar.copy(out=target[:, share:], in_=source[:, share:])
+        def cast_lower(c, g, shares):
+            target = w1_bf[c][:, g * pass_bf : (g + 1) * pass_bf].rearrange("p (a n t) -> p a t n", n=4, t=PACK)
+            source = w1_raw[(c, g)][:].rearrange("p t (a n) -> p a t n", n=4)
+            width = P // 4 // len(shares)
+            for n, copy in enumerate(shares):
+                copy(out=target[:, n * width : (n + 1) * width], in_=source[:, n * width : (n + 1) * width])
+
+        def cast_upper(g):
+            target = w1_bf_upper[:].rearrange("p (u g a e t) -> p g a t u e", u=2, g=PASSES, e=2, t=PACK)[:, g]
+            source = w1_raw[(2, g)][:].rearrange("p t (a u e) -> p a t u e", u=2, e=2)
+            width = P // 2 // 2
+            for n, copy in enumerate((on_vector, on_scalar)):
+                copy(out=target[:, n * width : (n + 1) * width], in_=source[:, n * width : (n + 1) * width])
+
+        def quantise_w1(c, g0, count):
+            source = w1_bf[c][:] if c < 2 else w1_bf_upper[:, (c - 2) * PASSES * pass_bf : (c - 1) * PASSES * pass_bf]
+            cols = slice(g0 * P, (g0 + count) * P)
+            nc.vector.quantize_mx(
+                out=w1_codes[c][:, cols].bitcast(FP8X4),
+                scales=w1_scales[c][:, cols],
+                in_=source[:, g0 * pass_bf : (g0 + count) * pass_bf],
+            )
 
         def project(c):
-            if c < 3:
-                count = 1 if c < 2 else 2
-                tile = keep.tile([P, count * width_bf], BF16, name=f"w1_bf{c}", tag=f"w1_bf{c}", align_bytes=64)
-                for n in range(count):
-                    w1_bf[c + n] = tile[:, n * width_bf : (n + 1) * width_bf]
-            codes = keep.tile([P, PASSES * P], U32, name=f"w1_codes{c}", align_bytes=64)
-            scales = keep.tile([P, PASSES * P], U8, name=f"w1_scales{c}", align_bytes=64)
-            for g in range(PASSES):
-                part = w1_bf[c][:, g * P * PACK : (g + 1) * P * PACK]
-                cast_w1(c, g, part)
-                if c == 0:
-                    cols = slice(g * P, (g + 1) * P)
-                    nc.vector.quantize_mx(out=codes[:, cols].bitcast(FP8X4), scales=scales[:, cols], in_=part)
-            if c > 0:
-                nc.vector.quantize_mx(out=codes[:].bitcast(FP8X4), scales=scales[:], in_=w1_bf[c])
             halves = [slice(s * HALF, (s + 1) * HALF) for s in range(2)]
-            pre = [psum.tile([P, HALF], F32, name=f"pre{c}_{s}", tag="acc", bufs=2) for s in range(2)]
+            if c < 2:
+                pre = [psum.tile([P, HALF], F32, name=f"pre{c}_{s}", tag="acc", bufs=2) for s in range(2)]
+            else:
+                tags = (("bh", "b2"), ("b3a", "b3b"))[c - 2]
+                pre = [psum.tile([P, HALF], F32, name=f"pre{c}_{s}", tag=tags[s]) for s in range(2)]
             if c == 0:
                 steps = [(g, s) for s in range(2) for g in range(PASSES)]
             else:
@@ -193,110 +153,112 @@ def tile_picked_wlapl_gelu_l_kernel(
                 cols = slice(g * P, (g + 1) * P)
                 nc.tensor.matmul_mx(
                     out=pre[s][:],
-                    lhsT=codes[:, cols].bitcast(FP8X4),
-                    lhsT_scale=scales[:, cols],
+                    lhsT=w1_codes[c][:, cols].bitcast(FP8X4),
+                    lhsT_scale=w1_scales[c][:, cols],
                     rhs=x_codes[s][:, g * HALF : (g + 1) * HALF].bitcast(FP8X4),
                     rhs_scale=x_planes[:, g * T : (g + 1) * T][:, halves[s]],
                     start=(g == 0),
                     stop=(g == PASSES - 1),
                 )
             for s in range(2):
-                nc.scalar.activation(
-                    out=h[c][:, halves[s]], in_=pre[s][:], func=GELU, bias=bias[c][:, :1] if c in bias else 0.0
+                nc.scalar.activation(out=h[c][:, halves[s]], in_=pre[s][:], func=GELU)
+
+        def negate_gate(d):
+            nc.vector.tensor_scalar(neg_gates[d][:], gates[d][:], -1.0, None, MULT)
+
+        def open_sums(tag, blocks, v0, width):
+            count = len(blocks) * width // P
+            tile = psum.tile([P, count * P], F32, name=f"sums_{tag}", tag=tag)
+            return [tile, blocks, v0, width, 0, count * (D + 1)]
+
+        def add_term(sums, c, term, term_v0):
+            tile, blocks, v0, width, done, total = sums
+            for b in range(width // P):
+                col = (b * len(blocks) + blocks.index(c)) * P
+                at = v0 + b * P - term_v0
+                nc.tensor.matmul(
+                    tile[:, col : col + P], term[:, at : at + P], ident[:],
+                    start=(done + b == 0), stop=(done + b == total - 1), is_transpose=True,
                 )
+            sums.insert(4, sums.pop(4) + width // P)
 
-        def negate(c):
-            if c in NEG_PLACE:
-                neg_h[c] = early.tile([P, T], F32, name=f"neg_h{c}", align_bytes=256, offset=NEG_PLACE[c])
-            else:
-                neg_h[c] = keep.tile([P, T], F32, name=f"neg_h{c}")
-            nc.scalar.activation(out=neg_h[c][:], in_=h[c][:, :T], func=COPY, scale=-1.0)
+        def place(kind, places, c, d, v0, width):
+            name = f"{kind}{c}_{d}_{v0}"
+            if (c, d) in places:
+                return early.tile([P, width], F32, name=name, align_bytes=256, offset=places[(c, d)])
+            return keep.tile([P, width], F32, name=name, align_bytes=64)
 
-        def neighbours(c, v0, width, pool, places, bank=None):
-            banks = range(v0 // P, (v0 + width) // P)
-            if bank is None:
-                sums = {b: zt[b][:, c * P : (c + 1) * P] for b in banks}
-                opens = closes = banks
-            else:
-                sums = {b: bank[:, b * P - v0 : (b + 1) * P - v0] for b in banks}
-                opens, closes = banks[:1], banks[-1:]
-            joins = 1 if c in NEG_PLACE else 0
-            for d in range(D):
-                if d == joins:
-                    for b in banks:
-                        nc.tensor.matmul(
-                            sums[b], neg_h[c][:, b * P : (b + 1) * P], ident[:],
-                            start=(d == 0 and b in opens), stop=False, is_transpose=True,
-                        )
-                name = f"prod{c}_{v0}_{d}"
-                if d in places:
-                    prod = pool.tile([P, width], F32, name=name, align_bytes=64, offset=places[d])
-                else:
-                    prod = keep.tile([P, width], F32, name=name, align_bytes=64)
-                nc.vector.tensor_tensor(
-                    prod[:],
-                    h[c][:].indirect(lists[d][:, v0 // 16 : (v0 + width) // 16]),
-                    gates[d][:, v0 : v0 + width],
-                    MULT,
-                )
-                for b in banks:
-                    nc.tensor.matmul(
-                        sums[b], prod[:, b * P - v0 : (b + 1) * P - v0], ident[:],
-                        start=(d < joins and b in opens), stop=(d == D - 1 and b in closes), is_transpose=True,
-                    )
+        def window(c, d, v0, width):
+            return h[c][:].indirect(lists[d][:, v0 // 16 : (v0 + width) // 16])
 
-        def late_places(first):
-            return {d: (first + d) * SMALL for d in range(D)}
+        def fused(sums, c, d):
+            v0, width = sums[2], sums[3]
+            prod = place("prod", PRODUCT_PLACE, c, d, v0, width)
+            nc.vector.tensor_tensor(prod[:], window(c, d, v0, width), neg_gates[d][:, v0 : v0 + width], MULT)
+            add_term(sums, c, prod, v0)
 
-        def round_z(c0, count, v0, width, bank=None, zero=None, on_vector=False):
+        fetched = {}
+
+        def fetch(c, d, v0, width):
+            tile = place("fetched", FETCH_PLACE, c, d, v0, width)
+            nc.scalar.activation(tile[:], window(c, d, v0, width), COPY)
             for b in range(v0 // P, (v0 + width) // P):
-                if bank is None:
-                    summed = zt[b][:, c0 * P : (c0 + count) * P]
-                else:
-                    summed = bank[:, b * P - v0 : (b + 1) * P - v0]
-                if c0 < 2:
-                    rows = slice(c0 * P // PACK, (c0 + count) * P // PACK)
-                    target = zt_bf[b][:].rearrange("v (u p e) -> v u p e", u=2, e=2)[:, :, rows, :]
-                    summed = summed.rearrange("v (p u e) -> v u p e", u=2, e=2)
-                else:
-                    target = zt_bf[b][:].rearrange("v (u s j) -> v u s j", u=2, s=2)[:, c0 - 2 : c0 - 2 + count, 1, :]
-                    summed = summed.rearrange("v (u j) -> v u j", u=count)
-                if on_vector:
-                    nc.vector.tensor_scalar(target, summed, -1.0, zero, MULT, ADD)
-                    continue
-                nc.scalar.activation(
-                    out=target,
-                    in_=summed,
-                    func=IDENTITY if zero is not None else COPY,
-                    bias=zero if zero is not None else 0.0,
-                    scale=-1.0,
-                )
+                fetched[(c, d, b)] = (tile, v0)
 
-        def turn_back(v0, z_bf, tag, parts=1):
-            turned = psum.tile([P, len(z_bf), 2, P], F32, name=f"turned{v0}", tag=tag)
-            for b in range(len(z_bf)):
-                words = zt_bf[v0 // P + b][:].bitcast(F32)
+        def weigh(sums, c, d):
+            v0, width = sums[2], sums[3]
+            tile, tile_v0 = fetched[(c, d, v0 // P)]
+            prod = place("prod", PRODUCT_PLACE, c, d, v0, width)
+            nc.vector.scalar_tensor_tensor(
+                prod[:], tile[:, v0 - tile_v0 : v0 - tile_v0 + width], -1.0, gates[d][:, v0 : v0 + width], MULT, MULT
+            )
+            add_term(sums, c, prod, v0)
+
+        def round_z(sums, copy):
+            tile, blocks, v0, width = sums[:4]
+            quarters = slice(v0 // P, (v0 + width) // P)
+            c = blocks[0]
+            if c < 2:
+                rows = slice(c * P // PACK, (c + 1) * P // PACK)
+                target = zt_bf[:].rearrange("v (b u p e) -> v b u p e", b=T // P, u=2, e=2)[:, quarters, :, rows, :]
+                summed = tile[:].rearrange("v (b p u e) -> v b u p e", b=width // P, u=2, e=2)
+            else:
+                target = zt_bf[:].rearrange("v (b u s j) -> v b u s j", b=T // P, u=2, s=2)
+                target = target[:, quarters, c - 2 : c - 2 + len(blocks), 1, :]
+                summed = tile[:].rearrange("v (b u j) -> v b u j", b=width // P, u=len(blocks))
+            copy(out=target, in_=summed)
+
+        def turn_back(v0, width, tag, parts):
+            count = width // P
+            turned = psum.tile([P, count, 2, P], F32, name=f"turned{v0}", tag=tag)
+            words = zt_bf[:].bitcast(F32)
+            for b in range(count):
                 for u in range(2):
-                    nc.tensor.transpose(turned[:, b, u, :], words[:, u * P : (u + 1) * P], ident[:])
-            width = P // parts
-            for b in range(len(z_bf)):
+                    at = (2 * (v0 // P + b) + u) * P
+                    nc.tensor.transpose(turned[:, b, u, :], words[:, at : at + P], ident[:])
+            z_bf = keep.tile([P, width * PACK], BF16, name=f"z_bf{v0}", align_bytes=64)
+            pairs = z_bf[:].bitcast(F32).rearrange("p (b v u) -> p b v u", b=count, u=2)
+            step = P // parts
+            for b in range(count):
                 for n in range(parts):
                     nc.scalar.copy(
-                        out=z_bf[b].bitcast(F32).rearrange("p (v u) -> p v u", u=2)[:, n * width : (n + 1) * width],
-                        in_=turned[:, b].rearrange("p u v -> p v u")[:, n * width : (n + 1) * width],
+                        out=pairs[:, b, n * step : (n + 1) * step],
+                        in_=turned[:, b].rearrange("p u v -> p v u")[:, n * step : (n + 1) * step],
                     )
+            return z_bf
 
-        def quantise_z(v0, z_bf, z_codes, parts=1):
-            z_scales = keep.tile([P, z_codes.shape[1]], U8, name=f"z_scales{v0}", align_bytes=64)
-            width = z_codes.shape[1] // parts
+        def quantise_z(v0, width, z_bf, parts):
+            z_codes = keep.tile([P, width], U32, name=f"z_codes{v0}", align_bytes=64)
+            z_scales = keep.tile([P, width], U8, name=f"z_scales{v0}", align_bytes=64)
+            step = width // parts
             for n in range(parts):
-                cols = slice(n * width, (n + 1) * width)
+                cols = slice(n * step, (n + 1) * step)
                 nc.vector.quantize_mx(
                     out=z_codes[:, cols].bitcast(FP8X4),
                     scales=z_scales[:, cols],
-                    in_=z_bf[:, n * width * PACK : (n + 1) * width * PACK],
+                    in_=z_bf[:, n * step * PACK : (n + 1) * step * PACK],
                 )
-            return z_codes, z_scales[:]
+            return z_codes[:], z_scales[:]
 
         def multiply(z_mx, m, acc):
             nc.tensor.matmul_mx(
@@ -316,62 +278,100 @@ def tile_picked_wlapl_gelu_l_kernel(
             copy_out(out=result[:].rearrange("p m v -> p (m v)"), in_=acc)
             nc.sync.dma_start(out=out_rows[:, m0 : m0 + count, v0 : v0 + width], in_=result[:])
 
-        on_scalar, on_vector = nc.scalar.copy, nc.vector.tensor_copy
-
+        cast_lower(0, 0, [on_vector])
+        quantise_w1(0, 0, 1)
+        cast_lower(0, 1, [on_vector, on_scalar])
+        quantise_w1(0, 1, 1)
         project(0)
+        cast_lower(1, 0, [on_vector])
+        negate_gate(0)
+        sums0 = open_sums("b0", [0], 0, T)
+        add_term(sums0, 0, h[0], 0)
+        fused(sums0, 0, 0)
+        fetch(0, 2, 0, T)
+        cast_lower(1, 1, [on_scalar])
+        quantise_w1(1, 0, PASSES)
+        negate_gate(1)
+        fetch(0, 3, 0, T)
         project(1)
-        negate(0)
-        neighbours(0, 0, T, early, PRODUCT_PLACE[0])
+        fused(sums0, 0, 1)
+        cast_upper(0)
+        weigh(sums0, 0, 2)
+        cast_upper(1)
+        weigh(sums0, 0, 3)
+        for c in (2, 3):
+            quantise_w1(c, 0, PASSES)
+
+        for d in range(FUSED, D):
+            fetch(1, d, 0, T)
         project(2)
         project(3)
-        for c in range(1, BLOCKS):
-            negate(c)
-        neighbours(1, 0, T, early, PRODUCT_PLACE[1])
-        round_z(0, 2, 0, T)
+        round_z(sums0, on_scalar)
+        sums1 = open_sums("b1", [1], 0, T)
+        add_term(sums1, 1, h[1], 0)
+        for d in range(FUSED):
+            fused(sums1, 1, d)
+        for d in range(FUSED, D):
+            weigh(sums1, 1, d)
 
+        upper = (2, 3)
         third, fourth = HALF, HALF + QUARTER
-        lower_sums = psum.tile([P, fourth], F32, tag="spare0")
-        neighbours(2, 0, fourth, late, {}, lower_sums[:])
-        round_z(2, 1, 0, fourth, lower_sums[:])
-        half_sums = psum.tile([P, HALF], F32, tag="spare1")
-        neighbours(3, 0, HALF, late, {}, half_sums[:])
-        round_z(3, 1, 0, HALF, half_sums[:], zero=half_bias[:, :1])
-        z_half = keep.tile([P, HALF * PACK], BF16, align_bytes=64)
-        turn_back(0, [z_half[:, : QUARTER * PACK], z_half[:, QUARTER * PACK :]], "zt0")
+        sums_half = open_sums("bh", [2, 3], 0, HALF)
+        sums2 = open_sums("b2", [2], HALF, HALF)
+        sums_third = open_sums("b3a", [3], third, QUARTER)
+        sums_fourth = open_sums("b3b", [3], fourth, QUARTER)
+        for c in upper:
+            add_term(sums_half, c, h[c], 0)
+        for c in upper:
+            for d in range(FUSED, D):
+                fetch(c, d, 0, HALF)
+        for c in upper:
+            for d in range(FUSED):
+                fused(sums_half, c, d)
+        add_term(sums2, 2, h[2], 0)
+        add_term(sums_third, 3, h[3], 0)
+        add_term(sums_fourth, 3, h[3], 0)
+        for c in upper:
+            for d in range(FUSED, D):
+                weigh(sums_half, c, d)
+        round_z(sums1, on_scalar)
+        for c in upper:
+            for d in range(FUSED, D):
+                fetch(c, d, HALF, HALF)
+        round_z(sums_half, on_scalar)
+        z_half = turn_back(0, HALF, "b0", 1)
 
-        third_sums = psum.tile([P, P], F32, tag="acc", bufs=2)
-        neighbours(3, third, QUARTER, late, late_places(0), third_sums[:])
-        round_z(3, 1, third, QUARTER, third_sums[:])
-        z_third = keep.tile([P, QUARTER * PACK], BF16, align_bytes=64)
-        turn_back(third, [z_third[:]], "spare0")
+        for sums, c in ((sums2, 2), (sums_third, 3)):
+            for d in range(FUSED):
+                fused(sums, c, d)
+            for d in range(FUSED, D):
+                weigh(sums, c, d)
+            round_z(sums, on_scalar)
+        z_third = turn_back(third, QUARTER, "b1", 1)
+        for d in range(FUSED):
+            fused(sums_fourth, 3, d)
+        for d in range(FUSED, D):
+            weigh(sums_fourth, 3, d)
 
-        neighbours(2, fourth, QUARTER, late, late_places(D))
-        round_z(2, 1, fourth, QUARTER)
-        last_sums = psum.tile([P, P], F32, tag="zt1")
-        neighbours(3, fourth, QUARTER, late, late_places(2 * D), last_sums[:])
-
-        codes_half = keep.tile([P, HALF], U32, tag=f"gate{D - 2}", align_bytes=256)
-        mx_half = quantise_z(0, z_half[:], codes_half[:])
+        mx_half = quantise_z(0, HALF, z_half, 1)
         acc_half0 = psum.tile([P, HALF], F32, tag="acc", bufs=2)
         multiply(mx_half, 0, acc_half0[:])
-        round_z(3, 1, fourth, QUARTER, last_sums[:], zero=last_bias[:], on_vector=True)
-        codes_third = keep.tile([P, QUARTER], U32, tag="codes_third", align_bytes=64)
-        mx_third = quantise_z(third, z_third[:], codes_third[:])
+        round_z(sums_fourth, on_vector)
+        mx_third = quantise_z(third, QUARTER, z_third, 1)
         store(0, HALF, 0, 1, acc_half0[:], on_vector)
-        z_fourth = keep.tile([P, QUARTER * PACK], BF16, align_bytes=64)
-        turn_back(fourth, [z_fourth[:]], "spare1", parts=2)
-        acc_half1 = psum.tile([P, HALF], F32, tag="zt1")
+        z_fourth = turn_back(fourth, QUARTER, "bh", 2)
+        acc_half1 = psum.tile([P, HALF], F32, tag="b3b")
         multiply(mx_half, 1, acc_half1[:])
         store(0, HALF, 1, 1, acc_half1[:], on_scalar)
-
-        acc_third = psum.tile([P, N // P * QUARTER], F32, tag="zt2")
+        acc_third = psum.tile([P, N // P * QUARTER], F32, tag="b2")
         for m in range(N // P):
             multiply(mx_third, m, acc_third[:, m * QUARTER : (m + 1) * QUARTER])
         store(third, QUARTER, 0, N // P, acc_third[:], on_scalar)
-
-        codes_fourth = keep.tile([P, QUARTER], U32, align_bytes=64)
-        mx_fourth = quantise_z(fourth, z_fourth[:], codes_fourth[:], parts=2)
+        mx_fourth = quantise_z(fourth, QUARTER, z_fourth, 2)
+        acc_fourth = [
+            psum.tile([P, QUARTER], F32, name="acc_fourth0", tag="acc", bufs=2),
+            psum.tile([P, QUARTER], F32, name="acc_fourth1", tag="b3a"),
+        ]
         for m, copy_out in enumerate((on_vector, on_scalar)):
-            acc = psum.tile([P, QUARTER], F32, name=f"acc_fourth{m}", tag="acc", bufs=2)
-            multiply(mx_fourth, m, acc[:])
-            store(fourth, QUARTER, m, 1, acc[:], copy_out)
+            multiply(mx_fourth, m, acc_fourth[m][:])
+            store(fourth, QUARTER, m, 1, acc_fourth[m][:], copy_out)

@@ -45,7 +45,7 @@ def tile_picked_wlapl_gelu_l_kernel(
         lists = [keep.tile([P, T // 16], U16, name=f"list{d}") for d in range(D)]
         gates = [keep.tile([P, T], F32, name=f"gate{d}", align_bytes=256) for d in range(D)]
         neg_gates = [keep.tile([P, T], F32, name=f"neg_gate{d}", align_bytes=256) for d in range(FUSED)]
-        x_codes = [keep.tile([P, PASSES * HALF], U32, name=f"x_codes{s}", align_bytes=256) for s in range(2)]
+        x_codes = keep.tile([P, PASSES * T], U32, align_bytes=256)
         x_planes = keep.tile([P, PASSES * T], U8, align_bytes=256)
         w2_codes = keep.tile([P, 2 * N], U8, align_bytes=64)
         w2_plane = keep.tile([P, N], U8, align_bytes=64)
@@ -85,7 +85,7 @@ def tile_picked_wlapl_gelu_l_kernel(
         x_rows = x_words.rearrange("g p n t -> p g (n t)").bitcast(I32)
         for s in range(2):
             nc.sync.dma_start(
-                out=x_codes[s][:].bitcast(I32).rearrange("p (g n) -> p g n", g=PASSES),
+                out=x_codes[:].bitcast(I32).rearrange("p (g n) -> p g n", g=PASSES)[:, :, s * HALF : (s + 1) * HALF],
                 in_=x_rows[:, :, s * HALF : (s + 1) * HALF],
             )
         load_w1(1, 0)
@@ -139,29 +139,26 @@ def tile_picked_wlapl_gelu_l_kernel(
             )
 
         def project(c):
-            halves = [slice(s * HALF, (s + 1) * HALF) for s in range(2)]
-            if c < 2:
-                pre = [psum.tile([P, HALF], F32, name=f"pre{c}_{s}", tag="acc", bufs=2) for s in range(2)]
-            else:
-                tags = (("bh", "b2"), ("b3a", "b3b"))[c - 2]
-                pre = [psum.tile([P, HALF], F32, name=f"pre{c}_{s}", tag=tags[s]) for s in range(2)]
-            if c == 0:
-                steps = [(g, s) for s in range(2) for g in range(PASSES)]
-            else:
-                steps = [(g, s) for g in range(PASSES) for s in range(2)]
-            for g, s in steps:
-                cols = slice(g * P, (g + 1) * P)
-                nc.tensor.matmul_mx(
-                    out=pre[s][:],
-                    lhsT=w1_codes[c][:, cols].bitcast(FP8X4),
-                    lhsT_scale=w1_scales[c][:, cols],
-                    rhs=x_codes[s][:, g * HALF : (g + 1) * HALF].bitcast(FP8X4),
-                    rhs_scale=x_planes[:, g * T : (g + 1) * T][:, halves[s]],
-                    start=(g == 0),
-                    stop=(g == PASSES - 1),
-                )
-            for s in range(2):
-                nc.scalar.activation(out=h[c][:, halves[s]], in_=pre[s][:], func=GELU)
+            parts = 2 if c < 2 else 1
+            width = T // parts
+            for s in range(parts):
+                if c < 2:
+                    pre = psum.tile([P, width], F32, name=f"pre{c}_{s}", tag="acc", bufs=2)
+                else:
+                    pre = psum.tile([P, width], F32, name=f"pre{c}", tag=("bh", "b3a")[c - 2])
+                for g in range(PASSES):
+                    cols = slice(g * P, (g + 1) * P)
+                    moving = slice(g * T + s * width, g * T + (s + 1) * width)
+                    nc.tensor.matmul_mx(
+                        out=pre[:],
+                        lhsT=w1_codes[c][:, cols].bitcast(FP8X4),
+                        lhsT_scale=w1_scales[c][:, cols],
+                        rhs=x_codes[:, moving].bitcast(FP8X4),
+                        rhs_scale=x_planes[:, moving],
+                        start=(g == 0),
+                        stop=(g == PASSES - 1),
+                    )
+                nc.scalar.activation(out=h[c][:, s * width : (s + 1) * width], in_=pre[:], func=GELU)
 
         def negate_gate(d):
             nc.vector.tensor_scalar(neg_gates[d][:], gates[d][:], -1.0, None, MULT)

from contextlib import ExitStack

import concourse.mybir as mybir
from concourse.masks import make_identity

K, T, D, H, N = 1024, 512, 4, 512, 256
FLOPS = 2 * K * H * T + 2 * H * N * T
BYTES = K * T + K * T // 32 + 4 * K * H + H * N // 2 + H * N // 32 + 4 * D * T + D * 128 * 64 + 4 * N * T

F32 = mybir.dt.float32
BF16 = mybir.dt.bfloat16
I32 = mybir.dt.int32
U32 = mybir.dt.uint32
U16 = mybir.dt.uint16
U8 = mybir.dt.uint8
FP8X4 = mybir.dt.float8_e4m3fn_x4
FP4X4 = mybir.dt.float4_e2m1fn_x4
GELU = mybir.ActivationFunctionType.Gelu_apprx_tanh
COPY = mybir.ActivationFunctionType.Copy
MULT = mybir.AluOpType.mult

P = 128
PACK = 4
PASSES = K // (P * PACK)
BLOCKS = H // P
HALF, QUARTER = T // 2, T // 4
SPARE = 8
FUSED = 2
UNIT = 4 * T

RAW_PLACE = {(0, 0): 0, (0, 1): UNIT, (1, 0): 2 * UNIT, (1, 1): 3 * UNIT, (2, 0): 4 * UNIT, (2, 1): 7 * UNIT}
PRODUCT_PLACE = {(0, 1): 3 * UNIT, (1, 0): 6 * UNIT + UNIT // 2, (1, 1): 8 * UNIT + UNIT // 2}
FETCH_PLACE = {(1, 2): 7 * UNIT + UNIT // 2, (0, 3): 10 * UNIT, (1, 3): 10 * UNIT}


def tile_picked_wlapl_gelu_l_kernel(
    tc, x_words, x_scales, w1, w2_words, w2_scales, gate, pos1, pos2, pos3, pos4, out
):
    nc = tc.nc
    with ExitStack() as ctx:
        keep = ctx.enter_context(tc.tile_pool(name="keep", bufs=1))
        early = ctx.enter_context(tc.tile_pool(name="early", bufs=1))
        psum = ctx.enter_context(tc.psum_pool(name="psum", bufs=1))

        lists = [keep.tile([P, T // 16], U16, name=f"list{d}") for d in range(D)]
        gates = [keep.tile([P, T], F32, name=f"gate{d}", align_bytes=256) for d in range(D)]
        neg_gates = [keep.tile([P, T], F32, name=f"neg_gate{d}", align_bytes=256) for d in range(FUSED)]
        x_codes = keep.tile([P, PASSES * T], U32, align_bytes=256)
        x_planes = keep.tile([P, PASSES * T], U8, align_bytes=256)
        w2_codes = keep.tile([P, 2 * N], U8, align_bytes=64)
        w2_plane = keep.tile([P, N], U8, align_bytes=64)
        ident = keep.tile([P, P], F32)
        zeros = keep.tile([P, SPARE], F32)
        h = [keep.tile([P, T + SPARE if c < 2 else T], F32, name=f"h{c}") for c in range(BLOCKS)]
        zt_bf = keep.tile([P, T // P * H], BF16, align_bytes=64)

        nc.gpsimd.memset(x_planes[:].bitcast(I32), 0)
        nc.vector.memset(zeros[:], 0.0)
        nc.vector.memset(w2_plane[:].bitcast(I32), 0)
        make_identity(nc, ident[:])

        w1_rows = w1.rearrange("(g p j) i -> g p j i", p=P, j=PACK)
        w1_raw = {}

        def load_w1(c, g):
            cols = slice(c * P, (c + 1) * P) if c < 2 else slice(2 * P, H)
            raw = early.tile(
                [P, PACK, cols.stop - cols.start], F32, name=f"w1_raw{c}_{g}", align_bytes=256, offset=RAW_PLACE[(c, g)]
            )
            nc.sync.dma_start(out=raw[:], in_=w1_rows[g][:, :, cols])
            w1_raw[(c, g)] = raw

        def load_list(d):
            nc.sync.dma_start(lists[d][:], (pos1, pos2, pos3, pos4)[d])

        def load_gate(d):
            nc.sync.dma_start(out=gates[d][:], in_=gate[d])

        load_w1(0, 0)
        load_w1(0, 1)
        x_plane_words = x_planes[:].bitcast(I32).rearrange("p (g w) -> p g w", g=PASSES)
        x_scale_rows = x_scales.bitcast(I32).rearrange("g (q r) w -> r q g w", r=4)
        for r in range(4):
            nc.sync.dma_start(out=x_plane_words[r:P:32], in_=x_scale_rows[r])
        x_rows = x_words.rearrange("g p n t -> p g (n t)").bitcast(I32)
        for s in range(2):
            nc.sync.dma_start(
                out=x_codes[:].bitcast(I32).rearrange("p (g n) -> p g n", g=PASSES)[:, :, s * HALF : (s + 1) * HALF],
                in_=x_rows[:, :, s * HALF : (s + 1) * HALF],
            )
        load_w1(1, 0)
        load_list(2)
        load_gate(0)
        load_list(0)
        load_w1(1, 1)
        load_list(3)
        load_gate(1)
        load_list(1)
        load_w1(2, 0)
        load_gate(2)
        load_w1(2, 1)
        load_gate(3)
        nc.sync.dma_start(out=w2_codes[:].bitcast(I32), in_=w2_words[0].bitcast(I32))
        w2_scale_rows = w2_scales[0].bitcast(I32).rearrange("(q r) w -> r q w", r=4)
        for r in range(4):
            nc.sync.dma_start(out=w2_plane[:].bitcast(I32)[r:P:32], in_=w2_scale_rows[r])

        for c in range(2):
            nc.scalar.activation(out=h[c][:, T:], in_=zeros[:], func=GELU)

        on_scalar, on_vector = nc.scalar.copy, nc.vector.tensor_copy
        pass_bf = P * PACK
        w1_bf = [keep.tile([P, PASSES * pass_bf], BF16, name=f"w1_bf{c}", align_bytes=64) for c in range(2)]
        w1_bf_upper = keep.tile([P, 2 * PASSES * pass_bf], BF16, align_bytes=64)
        w1_codes = [keep.tile([P, PASSES * P], U32, name=f"w1_codes{c}", align_bytes=64) for c in range(BLOCKS)]
        w1_scales = [keep.tile([P, PASSES * P], U8, name=f"w1_scales{c}", align_bytes=64) for c in range(BLOCKS)]

        def cast_lower(c, g, shares):
            target = w1_bf[c][:, g * pass_bf : (g + 1) * pass_bf].rearrange("p (a n t) -> p a t n", n=4, t=PACK)
            source = w1_raw[(c, g)][:].rearrange("p t (a n) -> p a t n", n=4)
            width = P // 4 // len(shares)
            for n, copy in enumerate(shares):
                copy(out=target[:, n * width : (n + 1) * width], in_=source[:, n * width : (n + 1) * width])

        def cast_upper(g):
            target = w1_bf_upper[:].rearrange("p (u g a e t) -> p g a t u e", u=2, g=PASSES, e=2, t=PACK)[:, g]
            source = w1_raw[(2, g)][:].rearrange("p t (a u e) -> p a t u e", u=2, e=2)
            width = P // 2 // 2
            for n, copy in enumerate((on_vector, on_scalar)):
                copy(out=target[:, n * width : (n + 1) * width], in_=source[:, n * width : (n + 1) * width])

        def quantise_w1(c, g0, count):
            source = w1_bf[c][:] if c < 2 else w1_bf_upper[:, (c - 2) * PASSES * pass_bf : (c - 1) * PASSES * pass_bf]
            cols = slice(g0 * P, (g0 + count) * P)
            nc.vector.quantize_mx(
                out=w1_codes[c][:, cols].bitcast(FP8X4),
                scales=w1_scales[c][:, cols],
                in_=source[:, g0 * pass_bf : (g0 + count) * pass_bf],
            )

        def project(c):
            parts = 2 if c < 2 else 1
            width = T // parts
            for s in range(parts):
                if c < 2:
                    pre = psum.tile([P, width], F32, name=f"pre{c}_{s}", tag="acc", bufs=2)
                else:
                    pre = psum.tile([P, width], F32, name=f"pre{c}", tag=("bh", "b3a")[c - 2])
                for g in range(PASSES):
                    cols = slice(g * P, (g + 1) * P)
                    moving = slice(g * T + s * width, g * T + (s + 1) * width)
                    nc.tensor.matmul_mx(
                        out=pre[:],
                        lhsT=w1_codes[c][:, cols].bitcast(FP8X4),
                        lhsT_scale=w1_scales[c][:, cols],
                        rhs=x_codes[:, moving].bitcast(FP8X4),
                        rhs_scale=x_planes[:, moving],
                        start=(g == 0),
                        stop=(g == PASSES - 1),
                    )
                nc.scalar.activation(out=h[c][:, s * width : (s + 1) * width], in_=pre[:], func=GELU)

        def negate_gate(d):
            nc.vector.tensor_scalar(neg_gates[d][:], gates[d][:], -1.0, None, MULT)

        def open_sums(tag, blocks, v0, width):
            count = len(blocks) * width // P
            tile = psum.tile([P, count * P], F32, name=f"sums_{tag}", tag=tag)
            return [tile, blocks, v0, width, 0, count * (D + 1)]

        def add_term(sums, c, term, term_v0):
            tile, blocks, v0, width, done, total = sums
            for b in range(width // P):
                col = (b * len(blocks) + blocks.index(c)) * P
                at = v0 + b * P - term_v0
                nc.tensor.matmul(
                    tile[:, col : col + P], term[:, at : at + P], ident[:],
                    start=(done + b == 0), stop=(done + b == total - 1), is_transpose=True,
                )
            sums.insert(4, sums.pop(4) + width // P)

        def place(kind, places, c, d, v0, width):
            name = f"{kind}{c}_{d}_{v0}"
            if (c, d) in places:
                return early.tile([P, width], F32, name=name, align_bytes=256, offset=places[(c, d)])
            return keep.tile([P, width], F32, name=name, align_bytes=64)

        def window(c, d, v0, width):
            return h[c][:].indirect(lists[d][:, v0 // 16 : (v0 + width) // 16])

        def fused(sums, c, d):
            v0, width = sums[2], sums[3]
            prod = place("prod", PRODUCT_PLACE, c, d, v0, width)
            nc.vector.tensor_tensor(prod[:], window(c, d, v0, width), neg_gates[d][:, v0 : v0 + width], MULT)
            add_term(sums, c, prod, v0)

        fetched = {}

        def fetch(c, d, v0, width):
            tile = place("fetched", FETCH_PLACE, c, d, v0, width)
            nc.scalar.activation(tile[:], window(c, d, v0, width), COPY)
            for b in range(v0 // P, (v0 + width) // P):
                fetched[(c, d, b)] = (tile, v0)

        def weigh(sums, c, d):
            v0, width = sums[2], sums[3]
            tile, tile_v0 = fetched[(c, d, v0 // P)]
            prod = place("prod", PRODUCT_PLACE, c, d, v0, width)
            nc.vector.scalar_tensor_tensor(
                prod[:], tile[:, v0 - tile_v0 : v0 - tile_v0 + width], -1.0, gates[d][:, v0 : v0 + width], MULT, MULT
            )
            add_term(sums, c, prod, v0)

        def round_z(sums, copy):
            tile, blocks, v0, width = sums[:4]
            quarters = slice(v0 // P, (v0 + width) // P)
            c = blocks[0]
            if c < 2:
                rows = slice(c * P // PACK, (c + 1) * P // PACK)
                target = zt_bf[:].rearrange("v (b u p e) -> v b u p e", b=T // P, u=2, e=2)[:, quarters, :, rows, :]
                summed = tile[:].rearrange("v (b p u e) -> v b u p e", b=width // P, u=2, e=2)
            else:
                target = zt_bf[:].rearrange("v (b u s j) -> v b u s j", b=T // P, u=2, s=2)
                target = target[:, quarters, c - 2 : c - 2 + len(blocks), 1, :]
                summed = tile[:].rearrange("v (b u j) -> v b u j", b=width // P, u=len(blocks))
            copy(out=target, in_=summed)

        def turn_back(v0, width, tag, parts):
            count = width // P
            turned = psum.tile([P, count, 2, P], F32, name=f"turned{v0}", tag=tag)
            words = zt_bf[:].bitcast(F32)
            for b in range(count):
                for u in range(2):
                    at = (2 * (v0 // P + b) + u) * P
                    nc.tensor.transpose(turned[:, b, u, :], words[:, at : at + P], ident[:])
            z_bf = keep.tile([P, width * PACK], BF16, name=f"z_bf{v0}", align_bytes=64)
            pairs = z_bf[:].bitcast(F32).rearrange("p (b v u) -> p b v u", b=count, u=2)
            step = P // parts
            for b in range(count):
                for n in range(parts):
                    nc.scalar.copy(
                        out=pairs[:, b, n * step : (n + 1) * step],
                        in_=turned[:, b].rearrange("p u v -> p v u")[:, n * step : (n + 1) * step],
                    )
            return z_bf

        def quantise_z(v0, width, z_bf, parts):
            z_codes = keep.tile([P, width], U32, name=f"z_codes{v0}", align_bytes=64)
            z_scales = keep.tile([P, width], U8, name=f"z_scales{v0}", align_bytes=64)
            step = width // parts
            for n in range(parts):
                cols = slice(n * step, (n + 1) * step)
                nc.vector.quantize_mx(
                    out=z_codes[:, cols].bitcast(FP8X4),
                    scales=z_scales[:, cols],
                    in_=z_bf[:, n * step * PACK : (n + 1) * step * PACK],
                )
            return z_codes[:], z_scales[:]

        def multiply(z_mx, m, acc):
            nc.tensor.matmul_mx(
                out=acc,
                lhsT=w2_codes[:, 2 * P * m : 2 * P * (m + 1)].bitcast(FP4X4),
                lhsT_scale=w2_plane[:, P * m : P * (m + 1)],
                rhs=z_mx[0].bitcast(FP8X4),
                rhs_scale=z_mx[1],
                start=True,
                stop=True,
            )

        out_rows = out.rearrange("(m p) v -> p m v", p=P)

        def store(v0, width, m0, count, acc, copy_out):
            result = keep.tile([P, count, width], F32, name=f"result{v0}_{m0}", align_bytes=256)
            copy_out(out=result[:].rearrange("p m v -> p (m v)"), in_=acc)
            nc.sync.dma_start(out=out_rows[:, m0 : m0 + count, v0 : v0 + width], in_=result[:])

        cast_lower(0, 0, [on_vector])
        quantise_w1(0, 0, 1)
        cast_lower(0, 1, [on_vector, on_scalar])
        quantise_w1(0, 1, 1)
        project(0)
        cast_lower(1, 0, [on_vector])
        negate_gate(0)
        sums0 = open_sums("b0", [0], 0, T)
        add_term(sums0, 0, h[0], 0)
        fused(sums0, 0, 0)
        fetch(0, 2, 0, T)
        cast_lower(1, 1, [on_scalar])
        quantise_w1(1, 0, PASSES)
        negate_gate(1)
        fetch(0, 3, 0, T)
        project(1)
        fused(sums0, 0, 1)
        cast_upper(0)
        weigh(sums0, 0, 2)
        cast_upper(1)
        weigh(sums0, 0, 3)
        for c in (2, 3):
            quantise_w1(c, 0, PASSES)

        for d in range(FUSED, D):
            fetch(1, d, 0, T)
        project(2)
        project(3)
        round_z(sums0, on_scalar)
        sums1 = open_sums("b1", [1], 0, T)
        add_term(sums1, 1, h[1], 0)
        for d in range(FUSED):
            fused(sums1, 1, d)
        for d in range(FUSED, D):
            weigh(sums1, 1, d)

        upper = (2, 3)
        third, fourth = HALF, HALF + QUARTER
        sums_half = open_sums("bh", [2, 3], 0, HALF)
        sums2 = open_sums("b2", [2], HALF, HALF)
        sums_third = open_sums("b3a", [3], third, QUARTER)
        sums_fourth = open_sums("b3b", [3], fourth, QUARTER)
        for c in upper:
            add_term(sums_half, c, h[c], 0)
        for c in upper:
            for d in range(FUSED, D):
                fetch(c, d, 0, HALF)
        for c in upper:
            for d in range(FUSED):
                fused(sums_half, c, d)
        add_term(sums2, 2, h[2], 0)
        add_term(sums_third, 3, h[3], 0)
        add_term(sums_fourth, 3, h[3], 0)
        for c in upper:
            for d in range(FUSED, D):
                weigh(sums_half, c, d)
        round_z(sums1, on_scalar)
        for c in upper:
            for d in range(FUSED, D):
                fetch(c, d, HALF, HALF)
        round_z(sums_half, on_scalar)
        z_half = turn_back(0, HALF, "b0", 1)

        for sums, c in ((sums2, 2), (sums_third, 3)):
            for d in range(FUSED):
                fused(sums, c, d)
            for d in range(FUSED, D):
                weigh(sums, c, d)
            round_z(sums, on_scalar)
        z_third = turn_back(third, QUARTER, "b1", 1)
        for d in range(FUSED):
            fused(sums_fourth, 3, d)
        for d in range(FUSED, D):
            weigh(sums_fourth, 3, d)

        mx_half = quantise_z(0, HALF, z_half, 1)
        acc_half0 = psum.tile([P, HALF], F32, tag="acc", bufs=2)
        multiply(mx_half, 0, acc_half0[:])
        round_z(sums_fourth, on_vector)
        mx_third = quantise_z(third, QUARTER, z_third, 1)
        store(0, HALF, 0, 1, acc_half0[:], on_vector)
        z_fourth = turn_back(fourth, QUARTER, "bh", 2)
        acc_half1 = psum.tile([P, HALF], F32, tag="b3b")
        multiply(mx_half, 1, acc_half1[:])
        store(0, HALF, 1, 1, acc_half1[:], on_scalar)
        acc_third = psum.tile([P, N // P * QUARTER], F32, tag="b2")
        for m in range(N // P):
            multiply(mx_third, m, acc_third[:, m * QUARTER : (m + 1) * QUARTER])
        store(third, QUARTER, 0, N // P, acc_third[:], on_scalar)
        mx_fourth = quantise_z(fourth, QUARTER, z_fourth, 2)
        acc_fourth = [
            psum.tile([P, QUARTER], F32, name="acc_fourth0", tag="acc", bufs=2),
            psum.tile([P, QUARTER], F32, name="acc_fourth1", tag="b3a"),
        ]
        for m, copy_out in enumerate((on_vector, on_scalar)):
            multiply(mx_fourth, m, acc_fourth[m][:])
            store(fourth, QUARTER, m, 1, acc_fourth[m][:], copy_out)
